import numpy as np
import ml_dtypes


def mxq(x, axis, fmt="e4m3"):
    dtype, down = {"e4m3": (ml_dtypes.float8_e4m3fn, 7), "e5m2": (ml_dtypes.float8_e5m2, 14)}[fmt]
    v = np.moveaxis(np.asarray(x, np.float32).astype(ml_dtypes.bfloat16).astype(np.float64), axis, -1)
    blocks = v.reshape(v.shape[:-1] + (-1, 32))
    amax = np.abs(blocks).max(-1, keepdims=True)
    byte = np.maximum(np.where(amax > 0, np.frexp(amax)[1] - 1 + 127, 0) - down, 1)
    scale = np.exp2(byte - 127.0)
    codes = (blocks / scale).astype(np.float32).astype(dtype).astype(np.float64)
    return np.moveaxis((codes * scale).reshape(v.shape), -1, axis)


WIDE = False


def mx_kscale(k):
    if not WIDE:
        return np.ones(k)
    levels = np.array([10, -10, 5, -5, 0])
    if k % 512:
        return np.exp2(np.random.permutation(np.resize(levels, k // 32))).repeat(32)
    a = np.empty((k // 512, 16))
    for p in range(k // 512):
        a[p, :8] = np.random.permutation(np.resize(levels, 8))
        for g in range(8):
            far = levels[np.abs(levels - a[p, g]) >= 10]
            a[p, g + 8] = far[np.random.randint(len(far))]
    return np.exp2(a.ravel()).repeat(32)


BF16 = ml_dtypes.bfloat16


def bf(x):
    return np.asarray(x, np.float32).astype(BF16)


def f64(x):
    return np.asarray(x).astype(np.float64)


E2M1 = np.array([0.0, 0.5, 1.0, 1.5, 2.0, 3.0, 4.0, 6.0, -0.0, -0.5, -1.0, -1.5, -2.0, -3.0, -4.0, -6.0])


def pack_weight(w, fmt):
    k, n = w.shape
    w = f64(bf(w)).reshape(k // 32, 32, n)
    amax = np.abs(w).max(1)
    if fmt == "e4m3":
        byte = np.frexp(amax)[1] - 1 + 127 - 7
    else:
        mant, ex = np.frexp(amax / 6.0)
        byte = np.where(mant > 0.5, ex, ex - 1) + 127
    byte = np.clip(np.where(amax > 0, byte, 1), 1, 254)
    scaled = (w * np.exp2(127.0 - byte)[:, None, :]).reshape(k, n).astype(np.float32)
    by_word = np.ascontiguousarray(scaled.reshape(k // 512, 128, 4, n).transpose(0, 1, 3, 2))
    if fmt == "e4m3":
        words = by_word.astype(ml_dtypes.float8_e4m3fn).view(np.uint8)
    else:
        c = by_word.astype(ml_dtypes.float4_e2m1fn).view(np.uint8) & 0xF
        words = c[..., 0::2] | (c[..., 1::2] << 4)
    return np.ascontiguousarray(words), np.ascontiguousarray(byte.astype(np.uint8).reshape(k // 512, 16, n))


def unpack_weight(words, scales, fmt):
    g, p, n, _ = words.shape
    if fmt == "e4m3":
        vals = np.ascontiguousarray(words).view(ml_dtypes.float8_e4m3fn).astype(np.float64)
    else:
        nib = np.empty((g, p, n, 4), np.uint8)
        nib[..., 0::2] = words & 0xF
        nib[..., 1::2] = words >> 4
        vals = E2M1[nib]
    vals = vals * np.repeat(np.exp2(scales.astype(np.float64) - 127.0), 8, axis=1)[..., None]
    return vals.transpose(0, 1, 3, 2).reshape(g * 512, n)
def pack4(w):
    words, scales = pack_weight(w, "e2m1")
    return words.reshape(words.shape[0], 128, -1), scales


def unpack4(words, scales):
    return unpack_weight(words.reshape(words.shape[0], 128, -1, 2), scales, "e2m1")


def planes(Y):
    n, m = Y.shape
    b = f64(bf(Y)).reshape(n // 32, 32, m)
    amax = np.abs(b).max(1)
    byte = np.clip(np.where(amax > 0, np.frexp(amax)[1] - 1 + 127 - 7, 1), 1, 254)
    codes = (b * np.exp2(127.0 - byte)[:, None, :]).reshape(n, m).astype(np.float32).astype(ml_dtypes.float8_e4m3fn).view(np.uint8)
    words = codes.reshape(n // 512, 128, 4, m).transpose(0, 1, 3, 2)
    return np.ascontiguousarray(words), np.ascontiguousarray(byte.astype(np.uint8).reshape(n // 512, 16, m))


N, D, F, L, Q = 1024, 1024, 1024, 512, 512


def setup_inputs():
    a, b, u = mx_kscale(D), mx_kscale(L), mx_kscale(N)
    lam = np.random.uniform(0.5, 1.5, F)
    x = bf(np.random.standard_normal((N, D)) * a)
    w_words, w_scales = pack4(np.random.standard_normal((D, F)) * lam / np.sqrt(D) / a[:, None])
    s = bf((1.0 + 0.3 * np.random.standard_normal(N)) * u)
    t = bf(np.random.standard_normal((N, Q)) / u[:, None])
    g = bf(np.random.standard_normal((N, L)) * b / u[:, None])
    beta_words, beta_scales = pack4(np.random.standard_normal((L, Q)) / np.sqrt(L) / b[:, None])
    tau = bf(np.random.uniform(0.5, 1.5, Q))
    return {
        "x": x,
        "w_words": w_words,
        "w_scales": w_scales,
        "s": s,
        "t": t,
        "g": g,
        "beta_words": beta_words,
        "beta_scales": beta_scales,
        "tau": tau,
    }


def candidate_nodes(x, w_words, w_scales):
    return np.tanh(mxq(f64(x), 1, "e4m3") @ unpack4(w_words, w_scales))


def network_residual(t, g, beta_words, beta_scales):
    return f64(t) - (mxq(f64(g), 1, "e4m3") @ unpack4(beta_words, beta_scales))


def core(x, w_words, w_scales, s, t, g, beta_words, beta_scales, tau):
    h = candidate_nodes(x, w_words, w_scales)
    e = network_residual(t, g, beta_words, beta_scales)
    hs = f64(s)[:, None] * h
    c = mxq(hs, 0, "e4m3").T @ mxq(e, 0, "e4m3")
    hh = np.sum(np.square(h), axis=0)
    return np.square(c) / hh[:, None] - f64(tau)[None, :]


def reference(x, w_words, w_scales, s, t, g, beta_words, beta_scales, tau):
    R_out = core(x, w_words, w_scales, s, t, g, beta_words, beta_scales, tau)
    words, scales = planes(R_out)
    return R_out, words, scales

@@ -1,0 +1,465 @@
+from contextlib import ExitStack
+
+import concourse.mybir as mybir
+from concourse.masks import make_identity
+
+N, D, F, L, Q = 1024, 1024, 1024, 512, 512
+FLOPS = 2 * (N * D * F + N * L * Q + F * N * Q)
+
+F32 = mybir.dt.float32
+BF16 = mybir.dt.bfloat16
+I32 = mybir.dt.int32
+U32 = mybir.dt.uint32
+U8 = mybir.dt.uint8
+FP8X4 = mybir.dt.float8_e4m3fn_x4
+FP4X4 = mybir.dt.float4_e2m1fn_x4
+ACT = mybir.ActivationFunctionType
+ALU = mybir.AluOpType
+
+P = 128
+FIRST = 1
+
+
+def tile_stochasticconfigurationcandidatescores_x2_kernel(
+    tc, x, w_words, w_scales, s, t, g, beta_words, beta_scales, tau, out_0, out_1, out_2
+):
+    nc = tc.nc
+    with ExitStack() as ctx:
+        keep = ctx.enter_context(tc.tile_pool(name="keep", bufs=1))
+        psum = ctx.enter_context(tc.psum_pool(name="psum", bufs=8))
+        ctx.enter_context(tc.manual_schedule())
+
+        def sb(name, shape, dtype):
+            return keep.tile(shape, dtype, name=name, align_bytes=64)
+
+        x_sb = [sb(f"x_sb{G}", [P, 4, D], BF16) for G in range(2)]
+        g_sb = [sb(f"g_sb{G}", [P, 4, L], BF16) for G in range(2)]
+        t_sb = [sb(f"t_sb{G}", [P, 4, Q], BF16) for G in range(2)]
+        w_sb = sb("w_sb", [P, 2, 2 * F], U8)
+        w_pl = sb("w_pl", [P, 2, F], U8)
+        b_sb = sb("b_sb", [P, 2 * Q], U8)
+        b_pl = sb("b_pl", [P, Q], U8)
+        s_sb = sb("s_sb", [P, 2, 4], BF16)
+        tau_sb = sb("tau_sb", [P, Q], BF16)
+        ident = sb("ident", [P, P], F32)
+        warm = sb("warm", [P, 1], F32)
+
+        nc.vector.memset(warm[:], 0.0)
+        nc.vector.memset(w_pl[:].rearrange("p g n -> p (g n)").bitcast(I32), 0)
+        nc.vector.memset(b_pl[:].bitcast(I32), 0)
+        make_identity(nc, ident[:])
+
+        x_hbm = x.rearrange("(G p t) d -> G p t d", G=2, t=4)
+        g_hbm = g.rearrange("(G p t) d -> G p t d", G=2, t=4)
+        t_hbm = t.rearrange("(G p t) d -> G p t d", G=2, t=4)
+        w_hbm = w_words.rearrange("g p n -> p g n")
+        w_sc = w_scales.rearrange("g q n -> q g n")
+
+        def load_x(G, ts):
+            nc.sync.dma_start(out=x_sb[G][:, ts, :], in_=x_hbm[G][:, ts, :])
+
+        def load_w(fh):
+            nc.sync.dma_start(
+                out=w_sb[:, :, F * fh : F * (fh + 1)].bitcast(I32),
+                in_=w_hbm[:, :, F * fh : F * (fh + 1)].bitcast(I32),
+            )
+
+        load_x(0, 0)
+        for q in range(4):
+            nc.sync.dma_start(
+                out=w_pl[32 * q : 32 * q + 4, :, :].bitcast(I32),
+                in_=w_sc[4 * q : 4 * q + 4, :, :].bitcast(I32),
+            )
+        load_w(FIRST)
+        for ts in range(1, 4):
+            load_x(0, ts)
+        for ts in range(4):
+            load_x(1, ts)
+        load_w(1 - FIRST)
+        nc.sync.dma_start(out=g_sb[1][:], in_=g_hbm[1])
+        for q in range(4):
+            nc.sync.dma_start(
+                out=b_pl[32 * q : 32 * q + 4, :].bitcast(I32),
+                in_=beta_scales[0][4 * q : 4 * q + 4, :].bitcast(I32),
+            )
+        nc.sync.dma_start(out=b_sb[:].bitcast(I32), in_=beta_words[0].bitcast(I32))
+        nc.sync.dma_start(out=g_sb[0][:], in_=g_hbm[0])
+        nc.sync.dma_start(out=t_sb[1][:], in_=t_hbm[1])
+        nc.sync.dma_start(out=t_sb[0][:], in_=t_hbm[0])
+        nc.sync.dma_start(out=tau_sb[:], in_=tau.partition_broadcast(P))
+        nc.gpsimd.dma_start(out=s_sb[:], in_=s.rearrange("(G p t) -> p G t", G=2, t=4))
+        nc.scalar.activation(out=warm[:], in_=warm[:], func=ACT.Tanh)
+
+        x_bf = [[sb(f"x_bf{G}{ts}", [P, 1024], BF16) for ts in range(4)] for G in range(2)]
+        x_cd = [[sb(f"x_cd{G}{ts}", [P, 2, P], U32) for ts in range(4)] for G in range(2)]
+        x_pl = [[sb(f"x_pl{G}{ts}", [P, 2, P], U8) for ts in range(4)] for G in range(2)]
+        g_bf = [sb(f"g_bf{G}", [P, 2048], BF16) for G in range(2)]
+        g_cd = [sb(f"g_cd{G}", [P, 4, P], U32) for G in range(2)]
+        g_pl = [sb(f"g_pl{G}", [P, 4, P], U8) for G in range(2)]
+        h = [[sb(f"h{G}{fh}", [P, 4, 512], F32) for fh in range(2)] for G in range(2)]
+        hs_bf = [[sb(f"hs_bf{G}{fh}", [P, 512, 4], BF16) for fh in range(2)] for G in range(2)]
+        hs_cd = [[sb(f"hs_cd{G}{fh}", [P, 512], U32) for fh in range(2)] for G in range(2)]
+        hs_pl = [[sb(f"hs_pl{G}{fh}", [P, 512], U8) for fh in range(2)] for G in range(2)]
+        e_bf = [sb(f"e_bf{G}", [P, 512, 4], BF16) for G in range(2)]
+        e_cd = [sb(f"e_cd{G}", [P, 512], U32) for G in range(2)]
+        e_pl = [sb(f"e_pl{G}", [P, 512], U8) for G in range(2)]
+        junk = [sb(f"junk{i}", [P, 512], F32) for i in range(2)]
+        acc = sb("acc", [P, 2, 8], F32)
+        hh = sb("hh", [P, 8], F32)
+        rhh = sb("rhh", [P, 8], F32)
+        sq = [sb(f"sq{fh}", [P, 4, 512], F32) for fh in range(2)]
+        o32 = [sb(f"o32{fh}", [P, 4, 512], F32) for fh in range(2)]
+        o_bf = [sb(f"o_bf{fh}", [P, 512, 4], BF16) for fh in range(2)]
+        o_cd = [sb(f"o_cd{fh}", [P, 512], U32) for fh in range(2)]
+        o_pl = [sb(f"o_pl{fh}", [P, 512], U8) for fh in range(2)]
+        banks = {}
+
+        def bank(key):
+            b = psum.tile([P, 512], F32, name="bank")
+            banks[key] = b
+            return b
+
+        def copy(eng, out, in_):
+            if eng == "v":
+                nc.vector.tensor_copy(out=out, in_=in_)
+            else:
+                nc.scalar.copy(out=out, in_=in_)
+
+        def x_t(G, ts):
+            b = bank(("x", G, ts))
+            words = x_sb[G][:, ts, :].bitcast(F32)
+            for k in range(2):
+                for u in range(2):
+                    i = 2 * k + u
+                    nc.tensor.transpose(b[:, P * i : P * (i + 1)], words[:, 256 * k + u : 256 * (k + 1) : 2], ident[:])
+
+        def x_c(G, ts, eng):
+            dst = x_bf[G][ts][:].bitcast(F32)
+            copy(
+                eng,
+                dst.rearrange("p (k r u) -> p k r u", k=2, u=2),
+                banks[("x", G, ts)][:].rearrange("p (k u r) -> p k r u", k=2, u=2),
+            )
+
+        def quant(cd, pl, src):
+            nc.vector.quantize_mx(out=cd.bitcast(FP8X4), scales=pl, in_=src)
+
+        def x_q(G, ts):
+            quant(
+                x_cd[G][ts][:].rearrange("p k r -> p (k r)"), x_pl[G][ts][:].rearrange("p k r -> p (k r)"), x_bf[G][ts][:]
+            )
+
+        def g_t(G, h2):
+            b = bank(("g", G, h2))
+            for j in range(2):
+                words = g_sb[G][:, 2 * h2 + j, :].bitcast(F32)
+                for u in range(2):
+                    i = 2 * j + u
+                    nc.tensor.transpose(b[:, P * i : P * (i + 1)], words[:, u:256:2], ident[:])
+
+        def g_c(G, h2, eng):
+            dst = g_bf[G][:].bitcast(F32)[:, 512 * h2 : 512 * (h2 + 1)]
+            copy(
+                eng,
+                dst.rearrange("p (j r u) -> p j r u", j=2, u=2),
+                banks[("g", G, h2)][:].rearrange("p (j u r) -> p j r u", j=2, u=2),
+            )
+
+        def g_q(G):
+            quant(g_cd[G][:].rearrange("p t r -> p (t r)"), g_pl[G][:].rearrange("p t r -> p (t r)"), g_bf[G][:])
+
+        def z_mm(G, fh, ts):
+            b = bank(("z", G, fh, ts))
+            for k in range(2):
+                nc.tensor.matmul_mx(
+                    out=b[:],
+                    lhsT=x_cd[G][ts][:, k, :].bitcast(FP8X4),
+                    lhsT_scale=x_pl[G][ts][:, k, :],
+                    rhs=w_sb[:, k, F * fh : F * (fh + 1)].bitcast(FP4X4),
+                    rhs_scale=w_pl[:, k, 512 * fh : 512 * (fh + 1)],
+                    start=(k == 0),
+                    stop=(k == 1),
+                )
+
+        def tanh(G, fh, ts):
+            nc.scalar.activation(
+                out=h[G][fh][:, ts, :].rearrange("p (j m) -> p j m", j=4),
+                in_=banks[("z", G, fh, ts)][:].rearrange("p (m j) -> p j m", j=4),
+                func=ACT.Tanh,
+            )
+
+        def h_t(G, fh, j):
+            b = bank(("h", G, fh, j))
+            for ts in range(4):
+                nc.tensor.transpose(b[:, P * ts : P * (ts + 1)], h[G][fh][:, ts, P * j : P * (j + 1)], ident[:])
+
+        def h_sq(G, fh, j):
+            k = 4 * fh + j
+            nc.scalar.activation(
+                out=junk[j % 2][:], in_=banks[("h", G, fh, j)][:], func=ACT.Square, accum_out=acc[:, G, k : k + 1]
+            )
+
+        def hs_mul(G, fh, lo, hi):
+            nc.vector.tensor_tensor(
+                out=hs_bf[G][fh][:, lo:hi, :],
+                in0=h[G][fh][:, :, lo:hi].rearrange("p t f -> p f t"),
+                in1=s_sb[:, G, :].unsqueeze(1).to_broadcast([P, hi - lo, 4]),
+                op=ALU.mult,
+            )
+
+        def hs_q(G, fh, lo, hi):
+            quant(
+                hs_cd[G][fh][:, lo:hi], hs_pl[G][fh][:, lo:hi], hs_bf[G][fh][:, lo:hi, :].rearrange("p f t -> p (f t)")
+            )
+
+        def e_mm(G, c):
+            b = bank(("e", G, c))
+            for ts in range(4):
+                nc.tensor.matmul_mx(
+                    out=b[:, P * ts : P * (ts + 1)],
+                    lhsT=g_cd[G][:, ts, :].bitcast(FP8X4),
+                    lhsT_scale=g_pl[G][:, ts, :],
+                    rhs=b_sb[:, 256 * c : 256 * (c + 1)].bitcast(FP4X4),
+                    rhs_scale=b_pl[:, P * c : P * (c + 1)],
+                    start=True,
+                    stop=True,
+                )
+
+        def e_sub(G, c):
+            nc.vector.tensor_tensor(
+                out=e_bf[G][:, P * c : P * (c + 1), :],
+                in0=t_sb[G][:, :, P * c : P * (c + 1)].rearrange("p t q -> p q t"),
+                in1=banks[("e", G, c)][:].rearrange("p (t q) -> p q t", t=4),
+                op=ALU.subtract,
+            )
+
+        def e_q(G):
+            quant(e_cd[G][:], e_pl[G][:], e_bf[G][:].rearrange("p q t -> p (q t)"))
+
+        def c_mm(fh, j):
+            b = bank(("c", fh, j))
+            for G in range(2):
+                nc.tensor.matmul_mx(
+                    out=b[:],
+                    lhsT=hs_cd[G][fh][:, P * j : P * (j + 1)].bitcast(FP8X4),
+                    lhsT_scale=hs_pl[G][fh][:, P * j : P * (j + 1)],
+                    rhs=e_cd[G][:].bitcast(FP8X4),
+                    rhs_scale=e_pl[G][:],
+                    start=(G == 0),
+                    stop=(G == 1),
+                )
+
+        def c_sq(fh, j):
+            nc.scalar.activation(out=sq[fh][:, j, :], in_=banks[("c", fh, j)][:], func=ACT.Square)
+
+        def hh_inv(fh):
+            k = slice(4 * fh, 4 * fh + 4)
+            nc.vector.tensor_tensor(out=hh[:, k], in0=acc[:, 0, k], in1=acc[:, 1, k], op=ALU.add)
+            nc.vector.reciprocal(out=rhh[:, k], in_=hh[:, k])
+
+        def c_out(fh, j):
+            k = 4 * fh + j
+            nc.vector.scalar_tensor_tensor(
+                out=o32[fh][:, j, :],
+                in0=sq[fh][:, j, :],
+                scalar=rhh[:, k : k + 1],
+                in1=tau_sb[:],
+                op0=ALU.mult,
+                op1=ALU.subtract,
+            )
+
+        def o_copy(fh, lo, hi, eng):
+            copy(eng, out=o_bf[fh][:, lo:hi, :], in_=o32[fh][:, :, lo:hi].rearrange("p j q -> p q j"))
+
+        def o_q(fh, lo, hi):
+            quant(o_cd[fh][:, lo:hi], o_pl[fh][:, lo:hi], o_bf[fh][:, lo:hi, :].rearrange("p q j -> p (q j)"))
+
+        def store_o(fh):
+            nc.sync.dma_start(
+                out=out_0[512 * fh : 512 * (fh + 1), :].rearrange("(p j) q -> p j q", j=4), in_=o32[fh][:]
+            )
+
+        def store_p(fh):
+            nc.sync.dma_start(
+                out=out_1[fh].rearrange("p m t -> p (m t)").bitcast(I32), in_=o_cd[fh][:].bitcast(I32)
+            )
+            for q in range(4):
+                nc.sync.dma_start(
+                    out=out_2[fh][4 * q : 4 * q + 4, :].bitcast(I32),
+                    in_=o_pl[fh][32 * q : 32 * q + 4, :].bitcast(I32),
+                )
+
+        x_t(0, 0)
+        x_c(0, 0, "s")
+        x_t(0, 1)
+        x_q(0, 0)
+        x_t(0, 2)
+        x_c(0, 1, "v")
+        x_t(0, 3)
+        x_c(0, 2, "s")
+        x_q(0, 1)
+        x_t(1, 0)
+        x_c(0, 3, "v")
+        x_t(1, 1)
+        x_q(0, 2)
+        x_t(1, 2)
+        x_q(0, 3)
+        x_c(1, 0, "v")
+        x_t(1, 3)
+        x_c(1, 1, "v")
+        z_mm(0, 1, 0)
+        x_c(1, 2, "v")
+        z_mm(0, 1, 1)
+        x_c(1, 3, "v")
+        tanh(0, 1, 0)
+        z_mm(0, 1, 2)
+        x_q(1, 0)
+        tanh(0, 1, 1)
+        x_q(1, 1)
+        z_mm(0, 1, 3)
+        tanh(0, 1, 2)
+        x_q(1, 2)
+        z_mm(1, 0, 0)
+        x_q(1, 3)
+        tanh(0, 1, 3)
+        z_mm(1, 0, 1)
+        tanh(1, 0, 0)
+        hs_mul(0, 1, 0, 128)
+        z_mm(1, 0, 2)
+        tanh(1, 0, 1)
+        hs_mul(0, 1, 128, 256)
+        z_mm(1, 0, 3)
+        tanh(1, 0, 2)
+        hs_mul(0, 1, 256, 384)
+        g_t(1, 0)
+        tanh(1, 0, 3)
+        hs_mul(0, 1, 384, 512)
+        g_t(1, 1)
+        g_c(1, 0, "s")
+        hs_mul(1, 0, 0, 128)
+        g_t(0, 0)
+        g_c(1, 1, "s")
+        hs_mul(1, 0, 128, 256)
+        g_t(0, 1)
+        g_c(0, 0, "s")
+        hs_mul(1, 0, 256, 384)
+        h_t(0, 1, 0)
+        h_t(0, 1, 1)
+        g_c(0, 1, "s")
+        hs_mul(1, 0, 384, 512)
+        h_t(0, 1, 2)
+        h_sq(0, 1, 0)
+        h_t(0, 1, 3)
+        g_q(0)
+        z_mm(1, 1, 0)
+        h_sq(0, 1, 1)
+        hs_q(1, 0, 0, 512)
+        z_mm(1, 1, 1)
+        h_sq(0, 1, 2)
+        g_q(1)
+        z_mm(1, 1, 2)
+        tanh(1, 1, 0)
+        hs_q(0, 1, 0, 512)
+        e_mm(1, 0)
+        tanh(1, 1, 1)
+        e_mm(1, 1)
+        e_sub(1, 0)
+        e_mm(1, 2)
+        tanh(1, 1, 2)
+        e_mm(1, 3)
+        e_sub(1, 1)
+        z_mm(1, 1, 3)
+        h_sq(0, 1, 3)
+        e_sub(1, 2)
+        z_mm(0, 0, 0)
+        tanh(1, 1, 3)
+        e_sub(1, 3)
+        z_mm(0, 0, 1)
+        tanh(0, 0, 0)
+        hs_mul(1, 1, 0, 128)
+        z_mm(0, 0, 2)
+        tanh(0, 0, 1)
+        hs_mul(1, 1, 128, 256)
+        z_mm(0, 0, 3)
+        tanh(0, 0, 2)
+        hs_mul(1, 1, 256, 384)
+        h_t(1, 1, 0)
+        tanh(0, 0, 3)
+        h_t(1, 1, 1)
+        hs_mul(1, 1, 384, 512)
+        h_t(1, 1, 2)
+        h_sq(1, 1, 0)
+        e_q(1)
+        h_t(0, 0, 0)
+        h_t(0, 0, 1)
+        h_sq(1, 1, 1)
+        hs_q(1, 1, 0, 512)
+        h_t(0, 0, 2)
+        h_t(0, 0, 3)
+        h_sq(1, 1, 2)
+        hs_mul(0, 0, 0, 128)
+        h_t(1, 1, 3)
+        e_mm(0, 0)
+        h_sq(0, 0, 0)
+        hs_mul(0, 0, 128, 256)
+        e_mm(0, 1)
+        hs_mul(0, 0, 256, 384)
+        h_sq(1, 1, 3)
+        e_mm(0, 2)
+        e_mm(0, 3)
+        e_sub(0, 0)
+        h_sq(0, 0, 1)
+        h_t(1, 0, 0)
+        e_sub(0, 1)
+        h_sq(0, 0, 2)
+        h_t(1, 0, 1)
+        h_t(1, 0, 2)
+        e_sub(0, 2)
+        h_sq(1, 0, 0)
+        h_t(1, 0, 3)
+        e_sub(0, 3)
+        h_sq(1, 0, 1)
+        hs_mul(0, 0, 384, 512)
+        h_sq(1, 0, 2)
+        e_q(0)
+        h_sq(1, 0, 3)
+        hs_q(0, 0, 0, 512)
+        c_mm(1, 0)
+        h_sq(0, 0, 3)
+        hh_inv(1)
+        c_mm(1, 1)
+        c_sq(1, 0)
+        hh_inv(0)
+        c_mm(1, 2)
+        c_sq(1, 1)
+        c_out(1, 0)
+        c_mm(1, 3)
+        c_sq(1, 2)
+        c_out(1, 1)
+        c_mm(0, 0)
+        c_sq(1, 3)
+        c_out(1, 2)
+        c_mm(0, 1)
+        c_sq(0, 0)
+        c_out(1, 3)
+        c_mm(0, 2)
+        c_sq(0, 1)
+        c_out(0, 0)
+        c_mm(0, 3)
+        store_o(1)
+        c_sq(0, 2)
+        c_out(0, 1)
+        c_sq(0, 3)
+        c_out(0, 2)
+        o_copy(1, 256, 512, "s")
+        c_out(0, 3)
+        o_copy(1, 0, 256, "v")
+        store_o(0)
+        o_copy(0, 0, 256, "s")
+        o_copy(0, 256, 512, "v")
+        o_q(1, 0, 256)
+        o_q(0, 256, 512)
+        o_q(0, 0, 256)
+        o_q(1, 256, 512)
+        store_p(0)
+        store_p(1)

@@ -17,7 +17,6 @@ ACT = mybir.ActivationFunctionType
 ALU = mybir.AluOpType
 
 P = 128
-FIRST = 1
 
 
 def tile_stochasticconfigurationcandidatescores_x2_kernel(
@@ -55,8 +54,8 @@ def tile_stochasticconfigurationcandidatescores_x2_kernel(
         w_hbm = w_words.rearrange("g p n -> p g n")
         w_sc = w_scales.rearrange("g q n -> q g n")
 
-        def load_x(G, ts):
-            nc.sync.dma_start(out=x_sb[G][:, ts, :], in_=x_hbm[G][:, ts, :])
+        def load_x(G, ts, te):
+            nc.sync.dma_start(out=x_sb[G][:, ts:te, :], in_=x_hbm[G][:, ts:te, :])
 
         def load_w(fh):
             nc.sync.dma_start(
@@ -64,29 +63,29 @@ def tile_stochasticconfigurationcandidatescores_x2_kernel(
                 in_=w_hbm[:, :, F * fh : F * (fh + 1)].bitcast(I32),
             )
 
-        load_x(0, 0)
-        for q in range(4):
-            nc.sync.dma_start(
-                out=w_pl[32 * q : 32 * q + 4, :, :].bitcast(I32),
-                in_=w_sc[4 * q : 4 * q + 4, :, :].bitcast(I32),
-            )
-        load_w(FIRST)
-        for ts in range(1, 4):
-            load_x(0, ts)
-        for ts in range(4):
-            load_x(1, ts)
-        load_w(1 - FIRST)
-        nc.sync.dma_start(out=g_sb[1][:], in_=g_hbm[1])
+        load_x(0, 0, 1)
+        load_w(0)
+        load_x(0, 1, 2)
+        load_x(0, 2, 4)
+        load_x(1, 0, 2)
+        load_x(1, 2, 4)
+        load_w(1)
+        nc.sync.dma_start(out=g_sb[0][:], in_=g_hbm[0])
         for q in range(4):
             nc.sync.dma_start(
                 out=b_pl[32 * q : 32 * q + 4, :].bitcast(I32),
                 in_=beta_scales[0][4 * q : 4 * q + 4, :].bitcast(I32),
             )
         nc.sync.dma_start(out=b_sb[:].bitcast(I32), in_=beta_words[0].bitcast(I32))
-        nc.sync.dma_start(out=g_sb[0][:], in_=g_hbm[0])
-        nc.sync.dma_start(out=t_sb[1][:], in_=t_hbm[1])
+        nc.sync.dma_start(out=g_sb[1][:], in_=g_hbm[1])
         nc.sync.dma_start(out=t_sb[0][:], in_=t_hbm[0])
+        nc.sync.dma_start(out=t_sb[1][:], in_=t_hbm[1])
         nc.sync.dma_start(out=tau_sb[:], in_=tau.partition_broadcast(P))
+        for q in range(4):
+            nc.scalar.dma_start(
+                out=w_pl[32 * q : 32 * q + 4, :, :].bitcast(I32),
+                in_=w_sc[4 * q : 4 * q + 4, :, :].bitcast(I32),
+            )
         nc.gpsimd.dma_start(out=s_sb[:], in_=s.rearrange("(G p t) -> p G t", G=2, t=4))
         nc.scalar.activation(out=warm[:], in_=warm[:], func=ACT.Tanh)
 
@@ -201,9 +200,9 @@ def tile_stochasticconfigurationcandidatescores_x2_kernel(
 
         def hs_mul(G, fh, lo, hi):
             nc.vector.tensor_tensor(
-                out=hs_bf[G][fh][:, lo:hi, :],
-                in0=h[G][fh][:, :, lo:hi].rearrange("p t f -> p f t"),
-                in1=s_sb[:, G, :].unsqueeze(1).to_broadcast([P, hi - lo, 4]),
+                out=hs_bf[G][fh][:, lo:hi, :].rearrange("p (c i) t -> p c t i", i=4),
+                in0=h[G][fh][:, :, lo:hi].rearrange("p t (c i) -> p c t i", i=4),
+                in1=s_sb[:, G, :].unsqueeze(1).unsqueeze(3).to_broadcast([P, (hi - lo) // 4, 4, 4]),
                 op=ALU.mult,
             )
 
@@ -227,9 +226,9 @@ def tile_stochasticconfigurationcandidatescores_x2_kernel(
 
         def e_sub(G, c):
             nc.vector.tensor_tensor(
-                out=e_bf[G][:, P * c : P * (c + 1), :],
-                in0=t_sb[G][:, :, P * c : P * (c + 1)].rearrange("p t q -> p q t"),
-                in1=banks[("e", G, c)][:].rearrange("p (t q) -> p q t", t=4),
+                out=e_bf[G][:, P * c : P * (c + 1), :].rearrange("p (b i) t -> p b t i", i=4),
+                in0=t_sb[G][:, :, P * c : P * (c + 1)].rearrange("p t (b i) -> p b t i", i=4),
+                in1=banks[("e", G, c)][:].rearrange("p (t b i) -> p b t i", t=4, i=4),
                 op=ALU.subtract,
             )
 
@@ -269,14 +268,20 @@ def tile_stochasticconfigurationcandidatescores_x2_kernel(
             )
 
         def o_copy(fh, lo, hi, eng):
-            copy(eng, out=o_bf[fh][:, lo:hi, :], in_=o32[fh][:, :, lo:hi].rearrange("p j q -> p q j"))
+            copy(
+                eng,
+                out=o_bf[fh][:, lo:hi, :].rearrange("p (b i) j -> p b j i", i=4),
+                in_=o32[fh][:, :, lo:hi].rearrange("p j (b i) -> p b j i", i=4),
+            )
 
         def o_q(fh, lo, hi):
             quant(o_cd[fh][:, lo:hi], o_pl[fh][:, lo:hi], o_bf[fh][:, lo:hi, :].rearrange("p q j -> p (q j)"))
 
-        def store_o(fh):
+        def store_o(fh, half):
+            js = slice(2 * half, 2 * half + 2)
             nc.sync.dma_start(
-                out=out_0[512 * fh : 512 * (fh + 1), :].rearrange("(p j) q -> p j q", j=4), in_=o32[fh][:]
+                out=out_0[512 * fh : 512 * (fh + 1), :].rearrange("(p j) q -> p j q", j=4)[:, js, :],
+                in_=o32[fh][:, js, :],
             )
 
         def store_p(fh):
@@ -291,175 +296,177 @@ def tile_stochasticconfigurationcandidatescores_x2_kernel(
 
         x_t(0, 0)
         x_c(0, 0, "s")
-        x_t(0, 1)
         x_q(0, 0)
-        x_t(0, 2)
+        x_t(0, 1)
         x_c(0, 1, "v")
-        x_t(0, 3)
-        x_c(0, 2, "s")
         x_q(0, 1)
-        x_t(1, 0)
-        x_c(0, 3, "v")
-        x_t(1, 1)
+        x_t(0, 2)
+        x_c(0, 2, "s")
         x_q(0, 2)
-        x_t(1, 2)
+        x_t(0, 3)
+        x_c(0, 3, "v")
         x_q(0, 3)
-        x_c(1, 0, "v")
-        x_t(1, 3)
-        x_c(1, 1, "v")
-        z_mm(0, 1, 0)
-        x_c(1, 2, "v")
-        z_mm(0, 1, 1)
-        x_c(1, 3, "v")
-        tanh(0, 1, 0)
-        z_mm(0, 1, 2)
-        x_q(1, 0)
-        tanh(0, 1, 1)
-        x_q(1, 1)
-        z_mm(0, 1, 3)
-        tanh(0, 1, 2)
-        x_q(1, 2)
-        z_mm(1, 0, 0)
-        x_q(1, 3)
-        tanh(0, 1, 3)
-        z_mm(1, 0, 1)
-        tanh(1, 0, 0)
-        hs_mul(0, 1, 0, 128)
-        z_mm(1, 0, 2)
-        tanh(1, 0, 1)
-        hs_mul(0, 1, 128, 256)
-        z_mm(1, 0, 3)
-        tanh(1, 0, 2)
-        hs_mul(0, 1, 256, 384)
-        g_t(1, 0)
-        tanh(1, 0, 3)
-        hs_mul(0, 1, 384, 512)
-        g_t(1, 1)
-        g_c(1, 0, "s")
-        hs_mul(1, 0, 0, 128)
-        g_t(0, 0)
-        g_c(1, 1, "s")
-        hs_mul(1, 0, 128, 256)
-        g_t(0, 1)
-        g_c(0, 0, "s")
-        hs_mul(1, 0, 256, 384)
-        h_t(0, 1, 0)
-        h_t(0, 1, 1)
-        g_c(0, 1, "s")
-        hs_mul(1, 0, 384, 512)
-        h_t(0, 1, 2)
-        h_sq(0, 1, 0)
-        h_t(0, 1, 3)
-        g_q(0)
-        z_mm(1, 1, 0)
-        h_sq(0, 1, 1)
-        hs_q(1, 0, 0, 512)
-        z_mm(1, 1, 1)
-        h_sq(0, 1, 2)
-        g_q(1)
-        z_mm(1, 1, 2)
-        tanh(1, 1, 0)
-        hs_q(0, 1, 0, 512)
-        e_mm(1, 0)
-        tanh(1, 1, 1)
-        e_mm(1, 1)
-        e_sub(1, 0)
-        e_mm(1, 2)
-        tanh(1, 1, 2)
-        e_mm(1, 3)
-        e_sub(1, 1)
-        z_mm(1, 1, 3)
-        h_sq(0, 1, 3)
-        e_sub(1, 2)
         z_mm(0, 0, 0)
-        tanh(1, 1, 3)
-        e_sub(1, 3)
-        z_mm(0, 0, 1)
         tanh(0, 0, 0)
-        hs_mul(1, 1, 0, 128)
-        z_mm(0, 0, 2)
+        z_mm(0, 0, 1)
         tanh(0, 0, 1)
-        hs_mul(1, 1, 128, 256)
-        z_mm(0, 0, 3)
+        z_mm(0, 0, 2)
         tanh(0, 0, 2)
-        hs_mul(1, 1, 256, 384)
-        h_t(1, 1, 0)
+        z_mm(0, 0, 3)
         tanh(0, 0, 3)
-        h_t(1, 1, 1)
-        hs_mul(1, 1, 384, 512)
-        h_t(1, 1, 2)
-        h_sq(1, 1, 0)
-        e_q(1)
-        h_t(0, 0, 0)
-        h_t(0, 0, 1)
-        h_sq(1, 1, 1)
-        hs_q(1, 1, 0, 512)
-        h_t(0, 0, 2)
-        h_t(0, 0, 3)
-        h_sq(1, 1, 2)
+        x_t(1, 0)
+        x_c(1, 0, "v")
+        x_t(1, 1)
+        x_c(1, 1, "v")
+        x_t(1, 2)
+        x_c(1, 2, "s")
+        x_t(1, 3)
+        x_c(1, 3, "s")
         hs_mul(0, 0, 0, 128)
-        h_t(1, 1, 3)
-        e_mm(0, 0)
-        h_sq(0, 0, 0)
+        x_q(1, 0)
         hs_mul(0, 0, 128, 256)
-        e_mm(0, 1)
+        x_q(1, 1)
         hs_mul(0, 0, 256, 384)
-        h_sq(1, 1, 3)
+        x_q(1, 2)
+        hs_mul(0, 0, 384, 512)
+        x_q(1, 3)
+        z_mm(0, 1, 0)
+        tanh(0, 1, 0)
+        z_mm(0, 1, 1)
+        tanh(0, 1, 1)
+        z_mm(0, 1, 2)
+        tanh(0, 1, 2)
+        z_mm(0, 1, 3)
+        tanh(0, 1, 3)
+        g_t(0, 0)
+        g_c(0, 0, "s")
+        g_t(0, 1)
+        g_c(0, 1, "s")
+        hs_mul(0, 1, 0, 128)
+        hs_mul(0, 1, 128, 256)
+        hs_mul(0, 1, 256, 384)
+        hs_mul(0, 1, 384, 512)
+        z_mm(1, 0, 0)
+        tanh(1, 0, 0)
+        z_mm(1, 0, 1)
+        tanh(1, 0, 1)
+        z_mm(1, 0, 2)
+        tanh(1, 0, 2)
+        z_mm(1, 0, 3)
+        tanh(1, 0, 3)
+        hs_q(0, 0, 0, 512)
+        g_q(0)
+        g_t(1, 0)
+        g_c(1, 0, "s")
+        g_t(1, 1)
+        g_c(1, 1, "s")
+        h_t(0, 0, 0)
+        h_sq(0, 0, 0)
+        h_t(0, 0, 1)
+        h_sq(0, 0, 1)
+        h_t(0, 0, 2)
+        h_sq(0, 0, 2)
+        h_t(0, 0, 3)
+        h_sq(0, 0, 3)
+        e_mm(0, 0)
+        e_mm(0, 1)
         e_mm(0, 2)
         e_mm(0, 3)
+        hs_mul(1, 0, 0, 128)
+        hs_mul(1, 0, 128, 256)
+        hs_mul(1, 0, 256, 384)
+        hs_mul(1, 0, 384, 512)
+        g_q(1)
+        h_t(0, 1, 0)
+        h_sq(0, 1, 0)
+        h_t(0, 1, 1)
+        h_sq(0, 1, 1)
+        h_t(0, 1, 2)
+        h_sq(0, 1, 2)
+        h_t(0, 1, 3)
+        h_sq(0, 1, 3)
         e_sub(0, 0)
-        h_sq(0, 0, 1)
-        h_t(1, 0, 0)
         e_sub(0, 1)
-        h_sq(0, 0, 2)
-        h_t(1, 0, 1)
-        h_t(1, 0, 2)
         e_sub(0, 2)
-        h_sq(1, 0, 0)
-        h_t(1, 0, 3)
         e_sub(0, 3)
-        h_sq(1, 0, 1)
-        hs_mul(0, 0, 384, 512)
-        h_sq(1, 0, 2)
+        hs_q(0, 1, 0, 512)
+        e_mm(1, 0)
+        e_sub(1, 0)
+        e_mm(1, 1)
+        e_sub(1, 1)
+        e_mm(1, 2)
+        e_sub(1, 2)
+        e_mm(1, 3)
+        e_sub(1, 3)
         e_q(0)
+        hs_q(1, 0, 0, 512)
+        z_mm(1, 1, 0)
+        tanh(1, 1, 0)
+        z_mm(1, 1, 1)
+        tanh(1, 1, 1)
+        z_mm(1, 1, 2)
+        tanh(1, 1, 2)
+        z_mm(1, 1, 3)
+        tanh(1, 1, 3)
+        h_t(1, 0, 0)
+        h_sq(1, 0, 0)
+        h_t(1, 0, 1)
+        h_sq(1, 0, 1)
+        h_t(1, 0, 2)
+        h_sq(1, 0, 2)
+        h_t(1, 0, 3)
         h_sq(1, 0, 3)
-        hs_q(0, 0, 0, 512)
-        c_mm(1, 0)
-        h_sq(0, 0, 3)
-        hh_inv(1)
-        c_mm(1, 1)
-        c_sq(1, 0)
-        hh_inv(0)
-        c_mm(1, 2)
-        c_sq(1, 1)
-        c_out(1, 0)
-        c_mm(1, 3)
-        c_sq(1, 2)
-        c_out(1, 1)
+        e_q(1)
+        hs_mul(1, 1, 0, 128)
+        hs_mul(1, 1, 128, 256)
+        hs_mul(1, 1, 256, 384)
+        hs_mul(1, 1, 384, 512)
         c_mm(0, 0)
-        c_sq(1, 3)
-        c_out(1, 2)
-        c_mm(0, 1)
         c_sq(0, 0)
-        c_out(1, 3)
-        c_mm(0, 2)
+        c_mm(0, 1)
         c_sq(0, 1)
-        c_out(0, 0)
-        c_mm(0, 3)
-        store_o(1)
+        c_mm(0, 2)
         c_sq(0, 2)
-        c_out(0, 1)
+        c_mm(0, 3)
         c_sq(0, 3)
+        hh_inv(0)
+        hs_q(1, 1, 0, 512)
+        c_out(0, 0)
+        c_out(0, 1)
         c_out(0, 2)
-        o_copy(1, 256, 512, "s")
         c_out(0, 3)
-        o_copy(1, 0, 256, "v")
-        store_o(0)
-        o_copy(0, 0, 256, "s")
+        store_o(0, 0)
+        store_o(0, 1)
+        h_t(1, 1, 0)
+        h_sq(1, 1, 0)
+        h_t(1, 1, 1)
+        h_sq(1, 1, 1)
+        h_t(1, 1, 2)
+        h_sq(1, 1, 2)
+        h_t(1, 1, 3)
+        h_sq(1, 1, 3)
+        c_mm(1, 0)
+        c_sq(1, 0)
+        c_mm(1, 1)
+        c_sq(1, 1)
+        c_mm(1, 2)
+        c_sq(1, 2)
+        c_mm(1, 3)
+        c_sq(1, 3)
         o_copy(0, 256, 512, "v")
-        o_q(1, 0, 256)
+        hh_inv(1)
+        o_copy(0, 0, 256, "s")
         o_q(0, 256, 512)
+        c_out(1, 0)
+        c_out(1, 1)
+        store_o(1, 0)
+        c_out(1, 2)
+        c_out(1, 3)
+        store_o(1, 1)
+        o_copy(1, 256, 512, "s")
+        o_copy(1, 0, 256, "v")
         o_q(0, 0, 256)
-        o_q(1, 256, 512)
         store_p(0)
+        o_q(1, 0, 256)
+        o_q(1, 256, 512)
         store_p(1)

@@ -42,7 +42,10 @@ def tile_stochasticconfigurationcandidatescores_x2_kernel(
         tau_sb = sb("tau_sb", [P, Q], BF16)
         ident = sb("ident", [P, P], F32)
         warm = sb("warm", [P, 1], F32)
+        zero = sb("zero", [P, 256], BF16)
+        x_wd = [sb(f"x_wd{ts}", [P, 512], I32) for ts in range(4)]
 
+        nc.vector.memset(zero[:], 0.0)
         nc.vector.memset(warm[:], 0.0)
         nc.vector.memset(w_pl[:].rearrange("p g n -> p (g n)").bitcast(I32), 0)
         nc.vector.memset(b_pl[:].bitcast(I32), 0)
@@ -70,6 +73,7 @@ def tile_stochasticconfigurationcandidatescores_x2_kernel(
         load_x(1, 0, 2)
         load_x(1, 2, 4)
         load_w(1)
+        nc.sync.dma_start(out=s_sb[:], in_=s.rearrange("(G p t) -> p G t", G=2, t=4))
         nc.sync.dma_start(out=g_sb[0][:], in_=g_hbm[0])
         for q in range(4):
             nc.sync.dma_start(
@@ -86,7 +90,6 @@ def tile_stochasticconfigurationcandidatescores_x2_kernel(
                 out=w_pl[32 * q : 32 * q + 4, :, :].bitcast(I32),
                 in_=w_sc[4 * q : 4 * q + 4, :, :].bitcast(I32),
             )
-        nc.gpsimd.dma_start(out=s_sb[:], in_=s.rearrange("(G p t) -> p G t", G=2, t=4))
         nc.scalar.activation(out=warm[:], in_=warm[:], func=ACT.Tanh)
 
         x_bf = [[sb(f"x_bf{G}{ts}", [P, 1024], BF16) for ts in range(4)] for G in range(2)]
@@ -124,13 +127,29 @@ def tile_stochasticconfigurationcandidatescores_x2_kernel(
             else:
                 nc.scalar.copy(out=out, in_=in_)
 
+        idle_bank = bank("idle")
+
+        def pe_idle(n):
+            for i in range(n):
+                nc.tensor.matmul(idle_bank[:, 0:256], lhsT=zero[:, 0:P], rhs=zero[:], start=True, stop=True)
+
+        def x_w(ts):
+            nc.gpsimd.tensor_copy(
+                out=x_wd[ts][:].rearrange("p (k u r) -> p k u r", k=2, u=2),
+                in_=x_sb[1][:, ts, :].bitcast(I32).rearrange("p (k r u) -> p k u r", k=2, u=2),
+            )
+
         def x_t(G, ts):
             b = bank(("x", G, ts))
             words = x_sb[G][:, ts, :].bitcast(F32)
             for k in range(2):
                 for u in range(2):
                     i = 2 * k + u
-                    nc.tensor.transpose(b[:, P * i : P * (i + 1)], words[:, 256 * k + u : 256 * (k + 1) : 2], ident[:])
+                    if G == 0:
+                        src = words[:, 256 * k + u : 256 * (k + 1) : 2]
+                    else:
+                        src = x_wd[ts][:, P * i : P * (i + 1)].bitcast(F32)
+                    nc.tensor.transpose(b[:, P * i : P * (i + 1)], src, ident[:])
 
         def x_c(G, ts, eng):
             dst = x_bf[G][ts][:].bitcast(F32)
@@ -256,13 +275,13 @@ def tile_stochasticconfigurationcandidatescores_x2_kernel(
             nc.vector.tensor_tensor(out=hh[:, k], in0=acc[:, 0, k], in1=acc[:, 1, k], op=ALU.add)
             nc.vector.reciprocal(out=rhh[:, k], in_=hh[:, k])
 
-        def c_out(fh, j):
+        def c_out(fh, j, lo, hi):
             k = 4 * fh + j
             nc.vector.scalar_tensor_tensor(
-                out=o32[fh][:, j, :],
-                in0=sq[fh][:, j, :],
+                out=o32[fh][:, j, lo:hi],
+                in0=sq[fh][:, j, lo:hi],
                 scalar=rhh[:, k : k + 1],
-                in1=tau_sb[:],
+                in1=tau_sb[:, lo:hi],
                 op0=ALU.mult,
                 op1=ALU.subtract,
             )
@@ -277,11 +296,10 @@ def tile_stochasticconfigurationcandidatescores_x2_kernel(
         def o_q(fh, lo, hi):
             quant(o_cd[fh][:, lo:hi], o_pl[fh][:, lo:hi], o_bf[fh][:, lo:hi, :].rearrange("p q j -> p (q j)"))
 
-        def store_o(fh, half):
-            js = slice(2 * half, 2 * half + 2)
+        def store_o(fh, lo, hi):
             nc.sync.dma_start(
-                out=out_0[512 * fh : 512 * (fh + 1), :].rearrange("(p j) q -> p j q", j=4)[:, js, :],
-                in_=o32[fh][:, js, :],
+                out=out_0[512 * fh : 512 * (fh + 1), :].rearrange("(p j) q -> p j q", j=4)[:, :, lo:hi],
+                in_=o32[fh][:, :, lo:hi],
             )
 
         def store_p(fh):
@@ -294,10 +312,17 @@ def tile_stochasticconfigurationcandidatescores_x2_kernel(
                     in_=o_pl[fh][32 * q : 32 * q + 4, :].bitcast(I32),
                 )
 
+        pe_idle(7)
+        x_w(0)
+        x_w(1)
+        x_w(2)
+        x_w(3)
         x_t(0, 0)
+        pe_idle(1)
         x_c(0, 0, "s")
         x_q(0, 0)
         x_t(0, 1)
+        pe_idle(1)
         x_c(0, 1, "v")
         x_q(0, 1)
         x_t(0, 2)
@@ -310,14 +335,14 @@ def tile_stochasticconfigurationcandidatescores_x2_kernel(
         tanh(0, 0, 0)
         z_mm(0, 0, 1)
         tanh(0, 0, 1)
-        z_mm(0, 0, 2)
-        tanh(0, 0, 2)
-        z_mm(0, 0, 3)
-        tanh(0, 0, 3)
         x_t(1, 0)
         x_c(1, 0, "v")
         x_t(1, 1)
         x_c(1, 1, "v")
+        z_mm(0, 0, 2)
+        tanh(0, 0, 2)
+        z_mm(0, 0, 3)
+        tanh(0, 0, 3)
         x_t(1, 2)
         x_c(1, 2, "s")
         x_t(1, 3)
@@ -431,12 +456,11 @@ def tile_stochasticconfigurationcandidatescores_x2_kernel(
         c_sq(0, 3)
         hh_inv(0)
         hs_q(1, 1, 0, 512)
-        c_out(0, 0)
-        c_out(0, 1)
-        c_out(0, 2)
-        c_out(0, 3)
-        store_o(0, 0)
-        store_o(0, 1)
+        c_out(0, 0, 0, 512)
+        c_out(0, 1, 0, 512)
+        c_out(0, 2, 0, 512)
+        c_out(0, 3, 0, 512)
+        store_o(0, 0, 512)
         h_t(1, 1, 0)
         h_sq(1, 1, 0)
         h_t(1, 1, 1)
@@ -453,19 +477,23 @@ def tile_stochasticconfigurationcandidatescores_x2_kernel(
         c_sq(1, 2)
         c_mm(1, 3)
         c_sq(1, 3)
-        o_copy(0, 256, 512, "v")
+        o_copy(0, 0, 256, "v")
         hh_inv(1)
-        o_copy(0, 0, 256, "s")
-        o_q(0, 256, 512)
-        c_out(1, 0)
-        c_out(1, 1)
-        store_o(1, 0)
-        c_out(1, 2)
-        c_out(1, 3)
-        store_o(1, 1)
-        o_copy(1, 256, 512, "s")
-        o_copy(1, 0, 256, "v")
+        o_copy(0, 256, 512, "s")
         o_q(0, 0, 256)
+        c_out(1, 0, 0, 256)
+        c_out(1, 1, 0, 256)
+        c_out(1, 2, 0, 256)
+        c_out(1, 3, 0, 256)
+        store_o(1, 0, 256)
+        c_out(1, 0, 256, 512)
+        c_out(1, 1, 256, 512)
+        c_out(1, 2, 256, 512)
+        c_out(1, 3, 256, 512)
+        store_o(1, 256, 512)
+        o_copy(1, 0, 256, "s")
+        o_copy(1, 256, 512, "v")
+        o_q(0, 256, 512)
         store_p(0)
         o_q(1, 0, 256)
         o_q(1, 256, 512)

@@ -40,16 +40,17 @@ def tile_stochasticconfigurationcandidatescores_x2_kernel(
         b_pl = sb("b_pl", [P, Q], U8)
         s_sb = sb("s_sb", [P, 2, 4], BF16)
         tau_sb = sb("tau_sb", [P, Q], BF16)
+        ones = sb("ones", [P, 256], BF16)
         ident = sb("ident", [P, P], F32)
         warm = sb("warm", [P, 1], F32)
-        zero = sb("zero", [P, 256], BF16)
         x_wd = [sb(f"x_wd{ts}", [P, 512], I32) for ts in range(4)]
 
-        nc.vector.memset(zero[:], 0.0)
+        nc.vector.memset(ones[:], 1.0)
         nc.vector.memset(warm[:], 0.0)
         nc.vector.memset(w_pl[:].rearrange("p g n -> p (g n)").bitcast(I32), 0)
         nc.vector.memset(b_pl[:].bitcast(I32), 0)
         make_identity(nc, ident[:])
+        nc.gpsimd.memset(tau_sb[:], 0.0)
 
         x_hbm = x.rearrange("(G p t) d -> G p t d", G=2, t=4)
         g_hbm = g.rearrange("(G p t) d -> G p t d", G=2, t=4)
@@ -84,7 +85,7 @@ def tile_stochasticconfigurationcandidatescores_x2_kernel(
         nc.sync.dma_start(out=g_sb[1][:], in_=g_hbm[1])
         nc.sync.dma_start(out=t_sb[0][:], in_=t_hbm[0])
         nc.sync.dma_start(out=t_sb[1][:], in_=t_hbm[1])
-        nc.sync.dma_start(out=tau_sb[:], in_=tau.partition_broadcast(P))
+        nc.sync.dma_start(out=tau_sb[0:1, :], in_=tau.unsqueeze(0))
         for q in range(4):
             nc.scalar.dma_start(
                 out=w_pl[32 * q : 32 * q + 4, :, :].bitcast(I32),
@@ -92,9 +93,9 @@ def tile_stochasticconfigurationcandidatescores_x2_kernel(
             )
         nc.scalar.activation(out=warm[:], in_=warm[:], func=ACT.Tanh)
 
-        x_bf = [[sb(f"x_bf{G}{ts}", [P, 1024], BF16) for ts in range(4)] for G in range(2)]
-        x_cd = [[sb(f"x_cd{G}{ts}", [P, 2, P], U32) for ts in range(4)] for G in range(2)]
-        x_pl = [[sb(f"x_pl{G}{ts}", [P, 2, P], U8) for ts in range(4)] for G in range(2)]
+        x_bf = [sb(f"x_bf{G}", [P, 4096], BF16) for G in range(2)]
+        x_cd = [sb(f"x_cd{G}", [P, 4, 2, P], U32) for G in range(2)]
+        x_pl = [sb(f"x_pl{G}", [P, 4, 2, P], U8) for G in range(2)]
         g_bf = [sb(f"g_bf{G}", [P, 2048], BF16) for G in range(2)]
         g_cd = [sb(f"g_cd{G}", [P, 4, P], U32) for G in range(2)]
         g_pl = [sb(f"g_pl{G}", [P, 4, P], U8) for G in range(2)]
@@ -131,7 +132,11 @@ def tile_stochasticconfigurationcandidatescores_x2_kernel(
 
         def pe_idle(n):
             for i in range(n):
-                nc.tensor.matmul(idle_bank[:, 0:256], lhsT=zero[:, 0:P], rhs=zero[:], start=True, stop=True)
+                nc.tensor.matmul(idle_bank[:, 0:256], lhsT=ones[:, 0:P], rhs=ones[:], start=True, stop=True)
+
+        def tau_mm():
+            b = bank("tau")
+            nc.tensor.matmul(b[:], lhsT=ones[:, 0:P], rhs=tau_sb[:], start=True, stop=True)
 
         def x_w(ts):
             nc.gpsimd.tensor_copy(
@@ -152,7 +157,7 @@ def tile_stochasticconfigurationcandidatescores_x2_kernel(
                     nc.tensor.transpose(b[:, P * i : P * (i + 1)], src, ident[:])
 
         def x_c(G, ts, eng):
-            dst = x_bf[G][ts][:].bitcast(F32)
+            dst = x_bf[G][:].bitcast(F32)[:, 512 * ts : 512 * (ts + 1)]
             copy(
                 eng,
                 dst.rearrange("p (k r u) -> p k r u", k=2, u=2),
@@ -162,9 +167,11 @@ def tile_stochasticconfigurationcandidatescores_x2_kernel(
         def quant(cd, pl, src):
             nc.vector.quantize_mx(out=cd.bitcast(FP8X4), scales=pl, in_=src)
 
-        def x_q(G, ts):
+        def x_q(G, ts, te):
             quant(
-                x_cd[G][ts][:].rearrange("p k r -> p (k r)"), x_pl[G][ts][:].rearrange("p k r -> p (k r)"), x_bf[G][ts][:]
+                x_cd[G][:, ts:te].rearrange("p t k r -> p (t k r)"),
+                x_pl[G][:, ts:te].rearrange("p t k r -> p (t k r)"),
+                x_bf[G][:, 1024 * ts : 1024 * te],
             )
 
         def g_t(G, h2):
@@ -191,8 +198,8 @@ def tile_stochasticconfigurationcandidatescores_x2_kernel(
             for k in range(2):
                 nc.tensor.matmul_mx(
                     out=b[:],
-                    lhsT=x_cd[G][ts][:, k, :].bitcast(FP8X4),
-                    lhsT_scale=x_pl[G][ts][:, k, :],
+                    lhsT=x_cd[G][:, ts, k, :].bitcast(FP8X4),
+                    lhsT_scale=x_pl[G][:, ts, k, :],
                     rhs=w_sb[:, k, F * fh : F * (fh + 1)].bitcast(FP4X4),
                     rhs_scale=w_pl[:, k, 512 * fh : 512 * (fh + 1)],
                     start=(k == 0),
@@ -281,35 +288,39 @@ def tile_stochasticconfigurationcandidatescores_x2_kernel(
                 out=o32[fh][:, j, lo:hi],
                 in0=sq[fh][:, j, lo:hi],
                 scalar=rhh[:, k : k + 1],
-                in1=tau_sb[:, lo:hi],
+                in1=banks["tau"][:, lo:hi],
                 op0=ALU.mult,
                 op1=ALU.subtract,
             )
 
         def o_copy(fh, lo, hi, eng):
-            copy(
-                eng,
-                out=o_bf[fh][:, lo:hi, :].rearrange("p (b i) j -> p b j i", i=4),
-                in_=o32[fh][:, :, lo:hi].rearrange("p j (b i) -> p b j i", i=4),
-            )
+            if eng == "g":
+                nc.gpsimd.tensor_copy(out=o_bf[fh][:, lo:hi, :], in_=o32[fh][:, :, lo:hi].rearrange("p j q -> p q j"))
+            else:
+                copy(
+                    eng,
+                    out=o_bf[fh][:, lo:hi, :].rearrange("p (b i) j -> p b j i", i=4),
+                    in_=o32[fh][:, :, lo:hi].rearrange("p j (b i) -> p b j i", i=4),
+                )
 
         def o_q(fh, lo, hi):
             quant(o_cd[fh][:, lo:hi], o_pl[fh][:, lo:hi], o_bf[fh][:, lo:hi, :].rearrange("p q j -> p (q j)"))
 
-        def store_o(fh, lo, hi):
+        def store_o(fh, js, je):
             nc.sync.dma_start(
-                out=out_0[512 * fh : 512 * (fh + 1), :].rearrange("(p j) q -> p j q", j=4)[:, :, lo:hi],
-                in_=o32[fh][:, :, lo:hi],
+                out=out_0[512 * fh : 512 * (fh + 1), :].rearrange("(p j) q -> p j q", j=4)[:, js:je, :],
+                in_=o32[fh][:, js:je, :],
             )
 
-        def store_p(fh):
+        def store_p(fh, lo, hi, eng):
             nc.sync.dma_start(
-                out=out_1[fh].rearrange("p m t -> p (m t)").bitcast(I32), in_=o_cd[fh][:].bitcast(I32)
+                out=out_1[fh][:, lo:hi, :].rearrange("p m t -> p (m t)").bitcast(I32),
+                in_=o_cd[fh][:, lo:hi].bitcast(I32),
             )
             for q in range(4):
-                nc.sync.dma_start(
-                    out=out_2[fh][4 * q : 4 * q + 4, :].bitcast(I32),
-                    in_=o_pl[fh][32 * q : 32 * q + 4, :].bitcast(I32),
+                eng.dma_start(
+                    out=out_2[fh][4 * q : 4 * q + 4, lo:hi].bitcast(I32),
+                    in_=o_pl[fh][32 * q : 32 * q + 4, lo:hi].bitcast(I32),
                 )
 
         pe_idle(7)
@@ -320,41 +331,37 @@ def tile_stochasticconfigurationcandidatescores_x2_kernel(
         x_t(0, 0)
         pe_idle(1)
         x_c(0, 0, "s")
-        x_q(0, 0)
+        x_q(0, 0, 1)
         x_t(0, 1)
         pe_idle(1)
-        x_c(0, 1, "v")
-        x_q(0, 1)
+        x_c(0, 1, "s")
+        x_q(0, 1, 2)
         x_t(0, 2)
         x_c(0, 2, "s")
-        x_q(0, 2)
+        x_q(0, 2, 3)
         x_t(0, 3)
-        x_c(0, 3, "v")
-        x_q(0, 3)
+        x_c(0, 3, "s")
+        x_q(0, 3, 4)
         z_mm(0, 0, 0)
         tanh(0, 0, 0)
         z_mm(0, 0, 1)
         tanh(0, 0, 1)
-        x_t(1, 0)
-        x_c(1, 0, "v")
-        x_t(1, 1)
-        x_c(1, 1, "v")
         z_mm(0, 0, 2)
         tanh(0, 0, 2)
         z_mm(0, 0, 3)
         tanh(0, 0, 3)
+        x_t(1, 0)
+        x_c(1, 0, "v")
+        x_t(1, 1)
+        x_c(1, 1, "v")
         x_t(1, 2)
         x_c(1, 2, "s")
         x_t(1, 3)
         x_c(1, 3, "s")
-        hs_mul(0, 0, 0, 128)
-        x_q(1, 0)
-        hs_mul(0, 0, 128, 256)
-        x_q(1, 1)
-        hs_mul(0, 0, 256, 384)
-        x_q(1, 2)
-        hs_mul(0, 0, 384, 512)
-        x_q(1, 3)
+        hs_mul(0, 0, 0, 256)
+        x_q(1, 0, 2)
+        hs_mul(0, 0, 256, 512)
+        x_q(1, 2, 4)
         z_mm(0, 1, 0)
         tanh(0, 1, 0)
         z_mm(0, 1, 1)
@@ -367,10 +374,8 @@ def tile_stochasticconfigurationcandidatescores_x2_kernel(
         g_c(0, 0, "s")
         g_t(0, 1)
         g_c(0, 1, "s")
-        hs_mul(0, 1, 0, 128)
-        hs_mul(0, 1, 128, 256)
-        hs_mul(0, 1, 256, 384)
-        hs_mul(0, 1, 384, 512)
+        hs_mul(0, 1, 0, 256)
+        hs_mul(0, 1, 256, 512)
         z_mm(1, 0, 0)
         tanh(1, 0, 0)
         z_mm(1, 0, 1)
@@ -397,10 +402,8 @@ def tile_stochasticconfigurationcandidatescores_x2_kernel(
         e_mm(0, 1)
         e_mm(0, 2)
         e_mm(0, 3)
-        hs_mul(1, 0, 0, 128)
-        hs_mul(1, 0, 128, 256)
-        hs_mul(1, 0, 256, 384)
-        hs_mul(1, 0, 384, 512)
+        hs_mul(1, 0, 0, 256)
+        hs_mul(1, 0, 256, 512)
         g_q(1)
         h_t(0, 1, 0)
         h_sq(0, 1, 0)
@@ -442,10 +445,9 @@ def tile_stochasticconfigurationcandidatescores_x2_kernel(
         h_t(1, 0, 3)
         h_sq(1, 0, 3)
         e_q(1)
-        hs_mul(1, 1, 0, 128)
-        hs_mul(1, 1, 128, 256)
-        hs_mul(1, 1, 256, 384)
-        hs_mul(1, 1, 384, 512)
+        hs_mul(1, 1, 0, 256)
+        hs_mul(1, 1, 256, 512)
+        tau_mm()
         c_mm(0, 0)
         c_sq(0, 0)
         c_mm(0, 1)
@@ -460,7 +462,7 @@ def tile_stochasticconfigurationcandidatescores_x2_kernel(
         c_out(0, 1, 0, 512)
         c_out(0, 2, 0, 512)
         c_out(0, 3, 0, 512)
-        store_o(0, 0, 512)
+        store_o(0, 0, 4)
         h_t(1, 1, 0)
         h_sq(1, 1, 0)
         h_t(1, 1, 1)
@@ -469,6 +471,7 @@ def tile_stochasticconfigurationcandidatescores_x2_kernel(
         h_sq(1, 1, 2)
         h_t(1, 1, 3)
         h_sq(1, 1, 3)
+        o_copy(0, 0, 256, "g")
         c_mm(1, 0)
         c_sq(1, 0)
         c_mm(1, 1)
@@ -477,24 +480,19 @@ def tile_stochasticconfigurationcandidatescores_x2_kernel(
         c_sq(1, 2)
         c_mm(1, 3)
         c_sq(1, 3)
-        o_copy(0, 0, 256, "v")
+        o_copy(0, 256, 512, "v")
         hh_inv(1)
-        o_copy(0, 256, 512, "s")
+        o_q(0, 256, 512)
+        c_out(1, 0, 0, 512)
+        c_out(1, 1, 0, 512)
         o_q(0, 0, 256)
-        c_out(1, 0, 0, 256)
-        c_out(1, 1, 0, 256)
-        c_out(1, 2, 0, 256)
-        c_out(1, 3, 0, 256)
-        store_o(1, 0, 256)
-        c_out(1, 0, 256, 512)
-        c_out(1, 1, 256, 512)
-        c_out(1, 2, 256, 512)
-        c_out(1, 3, 256, 512)
-        store_o(1, 256, 512)
+        store_p(0, 0, 512, nc.sync)
+        store_o(1, 0, 2)
+        c_out(1, 2, 0, 512)
+        c_out(1, 3, 0, 512)
+        store_o(1, 2, 4)
         o_copy(1, 0, 256, "s")
         o_copy(1, 256, 512, "v")
-        o_q(0, 256, 512)
-        store_p(0)
-        o_q(1, 0, 256)
         o_q(1, 256, 512)
-        store_p(1)
+        o_q(1, 0, 256)
+        store_p(1, 0, 512, nc.scalar)

@@ -3,8 +3,8 @@ from contextlib import ExitStack
 import concourse.mybir as mybir
 from concourse.masks import make_identity
 
-N, D, F, L, Q = 1024, 1024, 1024, 512, 512
-FLOPS = 2 * (N * D * F + N * L * Q + F * N * Q)
+N, D, H, L, Q = 1024, 1024, 1024, 512, 512
+FLOPS = 2 * (N * D * H + N * L * Q + H * N * Q)
 
 F32 = mybir.dt.float32
 BF16 = mybir.dt.bfloat16
@@ -17,6 +17,11 @@ ACT = mybir.ActivationFunctionType
 ALU = mybir.AluOpType
 
 P = 128
+T = 4
+GROUP = P * T
+BANK = 512
+GROUPS = range(2)
+TILES = range(T)
 
 
 def tile_stochasticconfigurationcandidatescores_x2_kernel(
@@ -28,45 +33,76 @@ def tile_stochasticconfigurationcandidatescores_x2_kernel(
         psum = ctx.enter_context(tc.psum_pool(name="psum", bufs=8))
         ctx.enter_context(tc.manual_schedule())
 
-        def sb(name, shape, dtype):
+        def sbuf(name, shape, dtype):
             return keep.tile(shape, dtype, name=name, align_bytes=64)
 
-        x_sb = [sb(f"x_sb{G}", [P, 4, D], BF16) for G in range(2)]
-        g_sb = [sb(f"g_sb{G}", [P, 4, L], BF16) for G in range(2)]
-        t_sb = [sb(f"t_sb{G}", [P, 4, Q], BF16) for G in range(2)]
-        w_sb = sb("w_sb", [P, 2, 2 * F], U8)
-        w_pl = sb("w_pl", [P, 2, F], U8)
-        b_sb = sb("b_sb", [P, 2 * Q], U8)
-        b_pl = sb("b_pl", [P, Q], U8)
-        s_sb = sb("s_sb", [P, 2, 4], BF16)
-        tau_sb = sb("tau_sb", [P, Q], BF16)
-        ones = sb("ones", [P, 256], BF16)
-        ident = sb("ident", [P, P], F32)
-        warm = sb("warm", [P, 1], F32)
-        x_wd = [sb(f"x_wd{ts}", [P, 512], I32) for ts in range(4)]
+        def bank():
+            return psum.tile([P, BANK], F32, name="bank")
 
+        x_in = [sbuf(f"x_in{G}", [P, T, D], BF16) for G in GROUPS]
+        x_words = sbuf("x_words", [P, T, BANK], I32)
+        g_in = [sbuf(f"g_in{G}", [P, T, L], BF16) for G in GROUPS]
+        t_in = [sbuf(f"t_in{G}", [P, T, Q], BF16) for G in GROUPS]
+        w_code = sbuf("w_code", [P, 2, 2 * H], U8)
+        w_scale = sbuf("w_scale", [P, 2, H], U8)
+        beta_code = sbuf("beta_code", [P, 2 * Q], U8)
+        beta_scale = sbuf("beta_scale", [P, Q], U8)
+        gain = sbuf("gain", [P, 2, T], BF16)
+        tau_row = sbuf("tau_row", [P, Q], BF16)
+        ones = sbuf("ones", [P, P], BF16)
+        ident = sbuf("ident", [P, P], F32)
+        zero = sbuf("zero", [P, 1], F32)
+
+        x_bf = [sbuf(f"x_bf{G}", [P, T * 2 * GROUP], BF16) for G in GROUPS]
+        x_code = [sbuf(f"x_code{G}", [P, T, 2, P], U32) for G in GROUPS]
+        x_scale = [sbuf(f"x_scale{G}", [P, T, 2, P], U8) for G in GROUPS]
+        g_bf = [sbuf(f"g_bf{G}", [P, T * GROUP], BF16) for G in GROUPS]
+        g_code = [sbuf(f"g_code{G}", [P, T, P], U32) for G in GROUPS]
+        g_scale = [sbuf(f"g_scale{G}", [P, T, P], U8) for G in GROUPS]
+        h = [[sbuf(f"h{G}{F}", [P, T, GROUP], F32) for F in GROUPS] for G in GROUPS]
+        hs_bf = [[sbuf(f"hs_bf{G}{F}", [P, GROUP, T], BF16) for F in GROUPS] for G in GROUPS]
+        hs_code = [[sbuf(f"hs_code{G}{F}", [P, GROUP], U32) for F in GROUPS] for G in GROUPS]
+        hs_scale = [[sbuf(f"hs_scale{G}{F}", [P, GROUP], U8) for F in GROUPS] for G in GROUPS]
+        e_bf = [sbuf(f"e_bf{G}", [P, Q, T], BF16) for G in GROUPS]
+        e_code = [sbuf(f"e_code{G}", [P, Q], U32) for G in GROUPS]
+        e_scale = [sbuf(f"e_scale{G}", [P, Q], U8) for G in GROUPS]
+
+        squares = [sbuf(f"squares{i}", [P, BANK], F32) for i in range(2)]
+        energy = sbuf("energy", [P, 2, 2 * T], F32)
+        hh = sbuf("hh", [P, 2 * T], F32)
+        inv_hh = sbuf("inv_hh", [P, 2 * T], F32)
+        c_sq = [sbuf(f"c_sq{F}", [P, T, Q], F32) for F in GROUPS]
+        out_f32 = [sbuf(f"out_f32{F}", [P, T, Q], F32) for F in GROUPS]
+        out_bf = [sbuf(f"out_bf{F}", [P, Q, T], BF16) for F in GROUPS]
+        out_code = [sbuf(f"out_code{F}", [P, Q], U32) for F in GROUPS]
+        out_scale = sbuf("out_scale", [P, 2, Q], U8)
+
+        nc.vector.memset(zero[:], 0.0)
+        nc.vector.memset(w_scale[:].rearrange("p k n -> p (k n)").bitcast(I32), 0)
+        nc.vector.memset(beta_scale[:].bitcast(I32), 0)
         nc.vector.memset(ones[:], 1.0)
-        nc.vector.memset(warm[:], 0.0)
-        nc.vector.memset(w_pl[:].rearrange("p g n -> p (g n)").bitcast(I32), 0)
-        nc.vector.memset(b_pl[:].bitcast(I32), 0)
         make_identity(nc, ident[:])
-        nc.gpsimd.memset(tau_sb[:], 0.0)
+        nc.gpsimd.memset(tau_row[:], 0.0)
 
-        x_hbm = x.rearrange("(G p t) d -> G p t d", G=2, t=4)
-        g_hbm = g.rearrange("(G p t) d -> G p t d", G=2, t=4)
-        t_hbm = t.rearrange("(G p t) d -> G p t d", G=2, t=4)
-        w_hbm = w_words.rearrange("g p n -> p g n")
-        w_sc = w_scales.rearrange("g q n -> q g n")
+        x_hbm = x.rearrange("(G p i) d -> G p i d", G=2, i=T)
+        g_hbm = g.rearrange("(G p i) d -> G p i d", G=2, i=T)
+        t_hbm = t.rearrange("(G p i) d -> G p i d", G=2, i=T)
+        w_hbm = w_words.rearrange("k p n -> p k n").bitcast(I32)
+        w_scale_hbm = w_scales.rearrange("k b n -> b k n").bitcast(I32)
 
-        def load_x(G, ts, te):
-            nc.sync.dma_start(out=x_sb[G][:, ts:te, :], in_=x_hbm[G][:, ts:te, :])
+        def load_x(G, lo, hi):
+            nc.sync.dma_start(out=x_in[G][:, lo:hi, :], in_=x_hbm[G][:, lo:hi, :])
 
-        def load_w(fh):
+        def load_w(F):
             nc.sync.dma_start(
-                out=w_sb[:, :, F * fh : F * (fh + 1)].bitcast(I32),
-                in_=w_hbm[:, :, F * fh : F * (fh + 1)].bitcast(I32),
+                out=w_code[:].bitcast(I32)[:, :, 256 * F : 256 * (F + 1)], in_=w_hbm[:, :, 256 * F : 256 * (F + 1)]
             )
 
+        for quad in range(4):
+            nc.scalar.dma_start(
+                out=w_scale[32 * quad : 32 * quad + 4, :, :].bitcast(I32),
+                in_=w_scale_hbm[4 * quad : 4 * quad + 4, :, :],
+            )
         load_x(0, 0, 1)
         load_w(0)
         load_x(0, 1, 2)
@@ -74,425 +110,266 @@ def tile_stochasticconfigurationcandidatescores_x2_kernel(
         load_x(1, 0, 2)
         load_x(1, 2, 4)
         load_w(1)
-        nc.sync.dma_start(out=s_sb[:], in_=s.rearrange("(G p t) -> p G t", G=2, t=4))
-        nc.sync.dma_start(out=g_sb[0][:], in_=g_hbm[0])
-        for q in range(4):
+        nc.sync.dma_start(out=gain[:], in_=s.rearrange("(G p i) -> p G i", G=2, i=T))
+        nc.sync.dma_start(out=g_in[0][:], in_=g_hbm[0])
+        for quad in range(4):
             nc.sync.dma_start(
-                out=b_pl[32 * q : 32 * q + 4, :].bitcast(I32),
-                in_=beta_scales[0][4 * q : 4 * q + 4, :].bitcast(I32),
+                out=beta_scale[32 * quad : 32 * quad + 4, :].bitcast(I32),
+                in_=beta_scales[0][4 * quad : 4 * quad + 4, :].bitcast(I32),
             )
-        nc.sync.dma_start(out=b_sb[:].bitcast(I32), in_=beta_words[0].bitcast(I32))
-        nc.sync.dma_start(out=g_sb[1][:], in_=g_hbm[1])
-        nc.sync.dma_start(out=t_sb[0][:], in_=t_hbm[0])
-        nc.sync.dma_start(out=t_sb[1][:], in_=t_hbm[1])
-        nc.sync.dma_start(out=tau_sb[0:1, :], in_=tau.unsqueeze(0))
-        for q in range(4):
-            nc.scalar.dma_start(
-                out=w_pl[32 * q : 32 * q + 4, :, :].bitcast(I32),
-                in_=w_sc[4 * q : 4 * q + 4, :, :].bitcast(I32),
-            )
-        nc.scalar.activation(out=warm[:], in_=warm[:], func=ACT.Tanh)
+        nc.sync.dma_start(out=beta_code[:].bitcast(I32), in_=beta_words[0].bitcast(I32))
+        nc.sync.dma_start(out=g_in[1][:], in_=g_hbm[1])
+        nc.sync.dma_start(out=t_in[0][:], in_=t_hbm[0])
+        nc.sync.dma_start(out=t_in[1][:], in_=t_hbm[1])
+        nc.sync.dma_start(out=tau_row[0:1, :], in_=tau.unsqueeze(0))
 
-        x_bf = [sb(f"x_bf{G}", [P, 4096], BF16) for G in range(2)]
-        x_cd = [sb(f"x_cd{G}", [P, 4, 2, P], U32) for G in range(2)]
-        x_pl = [sb(f"x_pl{G}", [P, 4, 2, P], U8) for G in range(2)]
-        g_bf = [sb(f"g_bf{G}", [P, 2048], BF16) for G in range(2)]
-        g_cd = [sb(f"g_cd{G}", [P, 4, P], U32) for G in range(2)]
-        g_pl = [sb(f"g_pl{G}", [P, 4, P], U8) for G in range(2)]
-        h = [[sb(f"h{G}{fh}", [P, 4, 512], F32) for fh in range(2)] for G in range(2)]
-        hs_bf = [[sb(f"hs_bf{G}{fh}", [P, 512, 4], BF16) for fh in range(2)] for G in range(2)]
-        hs_cd = [[sb(f"hs_cd{G}{fh}", [P, 512], U32) for fh in range(2)] for G in range(2)]
-        hs_pl = [[sb(f"hs_pl{G}{fh}", [P, 512], U8) for fh in range(2)] for G in range(2)]
-        e_bf = [sb(f"e_bf{G}", [P, 512, 4], BF16) for G in range(2)]
-        e_cd = [sb(f"e_cd{G}", [P, 512], U32) for G in range(2)]
-        e_pl = [sb(f"e_pl{G}", [P, 512], U8) for G in range(2)]
-        junk = [sb(f"junk{i}", [P, 512], F32) for i in range(2)]
-        acc = sb("acc", [P, 2, 8], F32)
-        hh = sb("hh", [P, 8], F32)
-        rhh = sb("rhh", [P, 8], F32)
-        sq = [sb(f"sq{fh}", [P, 4, 512], F32) for fh in range(2)]
-        o32 = [sb(f"o32{fh}", [P, 4, 512], F32) for fh in range(2)]
-        o_bf = [sb(f"o_bf{fh}", [P, 512, 4], BF16) for fh in range(2)]
-        o_cd = [sb(f"o_cd{fh}", [P, 512], U32) for fh in range(2)]
-        o_pl = [sb(f"o_pl{fh}", [P, 512], U8) for fh in range(2)]
-        banks = {}
-
-        def bank(key):
-            b = psum.tile([P, 512], F32, name="bank")
-            banks[key] = b
-            return b
+        nc.scalar.activation(out=zero[:], in_=zero[:], func=ACT.Tanh)
 
         def copy(eng, out, in_):
-            if eng == "v":
-                nc.vector.tensor_copy(out=out, in_=in_)
-            else:
+            if eng is nc.scalar:
                 nc.scalar.copy(out=out, in_=in_)
+            else:
+                nc.vector.tensor_copy(out=out, in_=in_)
 
-        idle_bank = bank("idle")
+        def quantize(code, scale, in_):
+            nc.vector.quantize_mx(out=code.bitcast(FP8X4), scales=scale, in_=in_)
 
-        def pe_idle(n):
-            for i in range(n):
-                nc.tensor.matmul(idle_bank[:, 0:256], lhsT=ones[:, 0:P], rhs=ones[:], start=True, stop=True)
-
-        def tau_mm():
-            b = bank("tau")
-            nc.tensor.matmul(b[:], lhsT=ones[:, 0:P], rhs=tau_sb[:], start=True, stop=True)
-
-        def x_w(ts):
+        def regroup_x(i):
             nc.gpsimd.tensor_copy(
-                out=x_wd[ts][:].rearrange("p (k u r) -> p k u r", k=2, u=2),
-                in_=x_sb[1][:, ts, :].bitcast(I32).rearrange("p (k r u) -> p k u r", k=2, u=2),
+                out=x_words[:, i, :].rearrange("p (k u r) -> p k u r", k=2, u=2),
+                in_=x_in[1][:, i, :].bitcast(I32).rearrange("p (k r u) -> p k u r", k=2, u=2),
             )
 
-        def x_t(G, ts):
-            b = bank(("x", G, ts))
-            words = x_sb[G][:, ts, :].bitcast(F32)
+        def turn_x(G, i):
+            b = bank()
+            words = x_in[G][:, i, :].bitcast(F32)
             for k in range(2):
                 for u in range(2):
-                    i = 2 * k + u
+                    n = 2 * k + u
                     if G == 0:
                         src = words[:, 256 * k + u : 256 * (k + 1) : 2]
                     else:
-                        src = x_wd[ts][:, P * i : P * (i + 1)].bitcast(F32)
-                    nc.tensor.transpose(b[:, P * i : P * (i + 1)], src, ident[:])
+                        src = x_words[:, i, P * n : P * (n + 1)].bitcast(F32)
+                    nc.tensor.transpose(b[:, P * n : P * (n + 1)], src, ident[:])
+            return b
 
-        def x_c(G, ts, eng):
-            dst = x_bf[G][:].bitcast(F32)[:, 512 * ts : 512 * (ts + 1)]
+        def turn_g(G, pair):
+            b = bank()
+            for n in range(4):
+                words = g_in[G][:, 2 * pair + n // 2, :].bitcast(F32)
+                nc.tensor.transpose(b[:, P * n : P * (n + 1)], words[:, n % 2 : 256 : 2], ident[:])
+            return b
+
+        def interleave(eng, bf, n, b):
             copy(
                 eng,
-                dst.rearrange("p (k r u) -> p k r u", k=2, u=2),
-                banks[("x", G, ts)][:].rearrange("p (k u r) -> p k r u", k=2, u=2),
+                out=bf[:].bitcast(F32)[:, BANK * n : BANK * (n + 1)].rearrange("p (a r u) -> p a r u", a=2, u=2),
+                in_=b[:].rearrange("p (a u r) -> p a r u", a=2, u=2),
             )
 
-        def quant(cd, pl, src):
-            nc.vector.quantize_mx(out=cd.bitcast(FP8X4), scales=pl, in_=src)
-
-        def x_q(G, ts, te):
-            quant(
-                x_cd[G][:, ts:te].rearrange("p t k r -> p (t k r)"),
-                x_pl[G][:, ts:te].rearrange("p t k r -> p (t k r)"),
-                x_bf[G][:, 1024 * ts : 1024 * te],
+        def quantize_x(G, lo, hi):
+            quantize(
+                x_code[G][:, lo:hi].rearrange("p i k r -> p (i k r)"),
+                x_scale[G][:, lo:hi].rearrange("p i k r -> p (i k r)"),
+                x_bf[G][:, 2 * GROUP * lo : 2 * GROUP * hi],
             )
 
-        def g_t(G, h2):
-            b = bank(("g", G, h2))
-            for j in range(2):
-                words = g_sb[G][:, 2 * h2 + j, :].bitcast(F32)
-                for u in range(2):
-                    i = 2 * j + u
-                    nc.tensor.transpose(b[:, P * i : P * (i + 1)], words[:, u:256:2], ident[:])
-
-        def g_c(G, h2, eng):
-            dst = g_bf[G][:].bitcast(F32)[:, 512 * h2 : 512 * (h2 + 1)]
-            copy(
-                eng,
-                dst.rearrange("p (j r u) -> p j r u", j=2, u=2),
-                banks[("g", G, h2)][:].rearrange("p (j u r) -> p j r u", j=2, u=2),
+        def quantize_g(G):
+            quantize(
+                g_code[G][:].rearrange("p i r -> p (i r)"), g_scale[G][:].rearrange("p i r -> p (i r)"), g_bf[G][:]
             )
 
-        def g_q(G):
-            quant(g_cd[G][:].rearrange("p t r -> p (t r)"), g_pl[G][:].rearrange("p t r -> p (t r)"), g_bf[G][:])
-
-        def z_mm(G, fh, ts):
-            b = bank(("z", G, fh, ts))
-            for k in range(2):
-                nc.tensor.matmul_mx(
-                    out=b[:],
-                    lhsT=x_cd[G][:, ts, k, :].bitcast(FP8X4),
-                    lhsT_scale=x_pl[G][:, ts, k, :],
-                    rhs=w_sb[:, k, F * fh : F * (fh + 1)].bitcast(FP4X4),
-                    rhs_scale=w_pl[:, k, 512 * fh : 512 * (fh + 1)],
-                    start=(k == 0),
-                    stop=(k == 1),
+        def nodes(G, F):
+            for i in TILES:
+                b = bank()
+                for k in range(2):
+                    nc.tensor.matmul_mx(
+                        out=b[:],
+                        lhsT=x_code[G][:, i, k, :].bitcast(FP8X4),
+                        lhsT_scale=x_scale[G][:, i, k, :],
+                        rhs=w_code[:, k, H * F : H * (F + 1)].bitcast(FP4X4),
+                        rhs_scale=w_scale[:, k, GROUP * F : GROUP * (F + 1)],
+                        start=(k == 0),
+                        stop=(k == 1),
+                    )
+                nc.scalar.activation(
+                    out=h[G][F][:, i, :].rearrange("p (j m) -> p j m", j=T),
+                    in_=b[:].rearrange("p (m j) -> p j m", j=T),
+                    func=ACT.Tanh,
+                    bias=zero[:, 0:1],
                 )
 
-        def tanh(G, fh, ts):
-            nc.scalar.activation(
-                out=h[G][fh][:, ts, :].rearrange("p (j m) -> p j m", j=4),
-                in_=banks[("z", G, fh, ts)][:].rearrange("p (m j) -> p j m", j=4),
-                func=ACT.Tanh,
-            )
-
-        def h_t(G, fh, j):
-            b = bank(("h", G, fh, j))
-            for ts in range(4):
-                nc.tensor.transpose(b[:, P * ts : P * (ts + 1)], h[G][fh][:, ts, P * j : P * (j + 1)], ident[:])
-
-        def h_sq(G, fh, j):
-            k = 4 * fh + j
-            nc.scalar.activation(
-                out=junk[j % 2][:], in_=banks[("h", G, fh, j)][:], func=ACT.Square, accum_out=acc[:, G, k : k + 1]
-            )
-
-        def hs_mul(G, fh, lo, hi):
+        def gain_nodes(G, F, half):
+            cols = slice(256 * half, 256 * (half + 1))
             nc.vector.tensor_tensor(
-                out=hs_bf[G][fh][:, lo:hi, :].rearrange("p (c i) t -> p c t i", i=4),
-                in0=h[G][fh][:, :, lo:hi].rearrange("p t (c i) -> p c t i", i=4),
-                in1=s_sb[:, G, :].unsqueeze(1).unsqueeze(3).to_broadcast([P, (hi - lo) // 4, 4, 4]),
+                out=hs_bf[G][F][:, cols, :].rearrange("p (c f) i -> p c i f", f=4),
+                in0=h[G][F][:, :, cols].rearrange("p i (c f) -> p c i f", f=4),
+                in1=gain[:, G, :].unsqueeze(1).unsqueeze(3).to_broadcast([P, 64, T, 4]),
                 op=ALU.mult,
             )
 
-        def hs_q(G, fh, lo, hi):
-            quant(
-                hs_cd[G][fh][:, lo:hi], hs_pl[G][fh][:, lo:hi], hs_bf[G][fh][:, lo:hi, :].rearrange("p f t -> p (f t)")
-            )
+        def quantize_hs(G, F):
+            quantize(hs_code[G][F][:], hs_scale[G][F][:], hs_bf[G][F][:].rearrange("p f i -> p (f i)"))
 
-        def e_mm(G, c):
-            b = bank(("e", G, c))
-            for ts in range(4):
+        def node_energy(G, F):
+            for j in TILES:
+                b = bank()
+                for i in TILES:
+                    nc.tensor.transpose(b[:, P * i : P * (i + 1)], h[G][F][:, i, P * j : P * (j + 1)], ident[:])
+                n = T * F + j
+                nc.scalar.activation(
+                    out=squares[j % 2][:], in_=b[:], func=ACT.Square, accum_out=energy[:, G, n : n + 1]
+                )
+
+        def invert_energy(F):
+            cols = slice(T * F, T * (F + 1))
+            nc.vector.tensor_tensor(out=hh[:, cols], in0=energy[:, 0, cols], in1=energy[:, 1, cols], op=ALU.add)
+            nc.vector.reciprocal(out=inv_hh[:, cols], in_=hh[:, cols])
+
+        def network(G, n):
+            b = bank()
+            for i in TILES:
                 nc.tensor.matmul_mx(
-                    out=b[:, P * ts : P * (ts + 1)],
-                    lhsT=g_cd[G][:, ts, :].bitcast(FP8X4),
-                    lhsT_scale=g_pl[G][:, ts, :],
-                    rhs=b_sb[:, 256 * c : 256 * (c + 1)].bitcast(FP4X4),
-                    rhs_scale=b_pl[:, P * c : P * (c + 1)],
+                    out=b[:, P * i : P * (i + 1)],
+                    lhsT=g_code[G][:, i, :].bitcast(FP8X4),
+                    lhsT_scale=g_scale[G][:, i, :],
+                    rhs=beta_code[:, 2 * P * n : 2 * P * (n + 1)].bitcast(FP4X4),
+                    rhs_scale=beta_scale[:, P * n : P * (n + 1)],
                     start=True,
                     stop=True,
                 )
+            return b
 
-        def e_sub(G, c):
+        def residual(G, n, b):
+            cols = slice(P * n, P * (n + 1))
             nc.vector.tensor_tensor(
-                out=e_bf[G][:, P * c : P * (c + 1), :].rearrange("p (b i) t -> p b t i", i=4),
-                in0=t_sb[G][:, :, P * c : P * (c + 1)].rearrange("p t (b i) -> p b t i", i=4),
-                in1=banks[("e", G, c)][:].rearrange("p (t b i) -> p b t i", t=4, i=4),
+                out=e_bf[G][:, cols, :].rearrange("p (c q) i -> p c i q", q=4),
+                in0=t_in[G][:, :, cols].rearrange("p i (c q) -> p c i q", q=4),
+                in1=b[:].rearrange("p (i c q) -> p c i q", i=T, q=4),
                 op=ALU.subtract,
             )
 
-        def e_q(G):
-            quant(e_cd[G][:], e_pl[G][:], e_bf[G][:].rearrange("p q t -> p (q t)"))
+        def quantize_e(G):
+            quantize(e_code[G][:], e_scale[G][:], e_bf[G][:].rearrange("p q i -> p (q i)"))
 
-        def c_mm(fh, j):
-            b = bank(("c", fh, j))
-            for G in range(2):
-                nc.tensor.matmul_mx(
-                    out=b[:],
-                    lhsT=hs_cd[G][fh][:, P * j : P * (j + 1)].bitcast(FP8X4),
-                    lhsT_scale=hs_pl[G][fh][:, P * j : P * (j + 1)],
-                    rhs=e_cd[G][:].bitcast(FP8X4),
-                    rhs_scale=e_pl[G][:],
-                    start=(G == 0),
-                    stop=(G == 1),
-                )
+        def correlate(F):
+            for j in TILES:
+                b = bank()
+                for G in GROUPS:
+                    nc.tensor.matmul_mx(
+                        out=b[:],
+                        lhsT=hs_code[G][F][:, P * j : P * (j + 1)].bitcast(FP8X4),
+                        lhsT_scale=hs_scale[G][F][:, P * j : P * (j + 1)],
+                        rhs=e_code[G][:].bitcast(FP8X4),
+                        rhs_scale=e_scale[G][:],
+                        start=(G == 0),
+                        stop=(G == 1),
+                    )
+                nc.scalar.activation(out=c_sq[F][:, j, :], in_=b[:], func=ACT.Square)
 
-        def c_sq(fh, j):
-            nc.scalar.activation(out=sq[fh][:, j, :], in_=banks[("c", fh, j)][:], func=ACT.Square)
-
-        def hh_inv(fh):
-            k = slice(4 * fh, 4 * fh + 4)
-            nc.vector.tensor_tensor(out=hh[:, k], in0=acc[:, 0, k], in1=acc[:, 1, k], op=ALU.add)
-            nc.vector.reciprocal(out=rhh[:, k], in_=hh[:, k])
-
-        def c_out(fh, j, lo, hi):
-            k = 4 * fh + j
+        def score(F, j):
+            n = T * F + j
             nc.vector.scalar_tensor_tensor(
-                out=o32[fh][:, j, lo:hi],
-                in0=sq[fh][:, j, lo:hi],
-                scalar=rhh[:, k : k + 1],
-                in1=banks["tau"][:, lo:hi],
+                out=out_f32[F][:, j, :],
+                in0=c_sq[F][:, j, :],
+                scalar=inv_hh[:, n : n + 1],
+                in1=tau_bank[:],
                 op0=ALU.mult,
                 op1=ALU.subtract,
             )
 
-        def o_copy(fh, lo, hi, eng):
-            if eng == "g":
-                nc.gpsimd.tensor_copy(out=o_bf[fh][:, lo:hi, :], in_=o32[fh][:, :, lo:hi].rearrange("p j q -> p q j"))
-            else:
-                copy(
-                    eng,
-                    out=o_bf[fh][:, lo:hi, :].rearrange("p (b i) j -> p b j i", i=4),
-                    in_=o32[fh][:, :, lo:hi].rearrange("p j (b i) -> p b j i", i=4),
-                )
-
-        def o_q(fh, lo, hi):
-            quant(o_cd[fh][:, lo:hi], o_pl[fh][:, lo:hi], o_bf[fh][:, lo:hi, :].rearrange("p q j -> p (q j)"))
-
-        def store_o(fh, js, je):
+        def store_scores(F, lo, hi):
             nc.sync.dma_start(
-                out=out_0[512 * fh : 512 * (fh + 1), :].rearrange("(p j) q -> p j q", j=4)[:, js:je, :],
-                in_=o32[fh][:, js:je, :],
+                out=out_0[GROUP * F : GROUP * (F + 1), :].rearrange("(p j) q -> p j q", j=T)[:, lo:hi, :],
+                in_=out_f32[F][:, lo:hi, :],
             )
 
-        def store_p(fh, lo, hi, eng):
-            nc.sync.dma_start(
-                out=out_1[fh][:, lo:hi, :].rearrange("p m t -> p (m t)").bitcast(I32),
-                in_=o_cd[fh][:, lo:hi].bitcast(I32),
+        def round_scores(eng, F, half):
+            cols = slice(256 * half, 256 * (half + 1))
+            copy(
+                eng,
+                out=out_bf[F][:, cols, :].rearrange("p (c q) j -> p c j q", q=4),
+                in_=out_f32[F][:, :, cols].rearrange("p j (c q) -> p c j q", q=4),
             )
-            for q in range(4):
-                eng.dma_start(
-                    out=out_2[fh][4 * q : 4 * q + 4, lo:hi].bitcast(I32),
-                    in_=o_pl[fh][32 * q : 32 * q + 4, lo:hi].bitcast(I32),
-                )
 
-        pe_idle(7)
-        x_w(0)
-        x_w(1)
-        x_w(2)
-        x_w(3)
-        x_t(0, 0)
-        pe_idle(1)
-        x_c(0, 0, "s")
-        x_q(0, 0, 1)
-        x_t(0, 1)
-        pe_idle(1)
-        x_c(0, 1, "s")
-        x_q(0, 1, 2)
-        x_t(0, 2)
-        x_c(0, 2, "s")
-        x_q(0, 2, 3)
-        x_t(0, 3)
-        x_c(0, 3, "s")
-        x_q(0, 3, 4)
-        z_mm(0, 0, 0)
-        tanh(0, 0, 0)
-        z_mm(0, 0, 1)
-        tanh(0, 0, 1)
-        z_mm(0, 0, 2)
-        tanh(0, 0, 2)
-        z_mm(0, 0, 3)
-        tanh(0, 0, 3)
-        x_t(1, 0)
-        x_c(1, 0, "v")
-        x_t(1, 1)
-        x_c(1, 1, "v")
-        x_t(1, 2)
-        x_c(1, 2, "s")
-        x_t(1, 3)
-        x_c(1, 3, "s")
-        hs_mul(0, 0, 0, 256)
-        x_q(1, 0, 2)
-        hs_mul(0, 0, 256, 512)
-        x_q(1, 2, 4)
-        z_mm(0, 1, 0)
-        tanh(0, 1, 0)
-        z_mm(0, 1, 1)
-        tanh(0, 1, 1)
-        z_mm(0, 1, 2)
-        tanh(0, 1, 2)
-        z_mm(0, 1, 3)
-        tanh(0, 1, 3)
-        g_t(0, 0)
-        g_c(0, 0, "s")
-        g_t(0, 1)
-        g_c(0, 1, "s")
-        hs_mul(0, 1, 0, 256)
-        hs_mul(0, 1, 256, 512)
-        z_mm(1, 0, 0)
-        tanh(1, 0, 0)
-        z_mm(1, 0, 1)
-        tanh(1, 0, 1)
-        z_mm(1, 0, 2)
-        tanh(1, 0, 2)
-        z_mm(1, 0, 3)
-        tanh(1, 0, 3)
-        hs_q(0, 0, 0, 512)
-        g_q(0)
-        g_t(1, 0)
-        g_c(1, 0, "s")
-        g_t(1, 1)
-        g_c(1, 1, "s")
-        h_t(0, 0, 0)
-        h_sq(0, 0, 0)
-        h_t(0, 0, 1)
-        h_sq(0, 0, 1)
-        h_t(0, 0, 2)
-        h_sq(0, 0, 2)
-        h_t(0, 0, 3)
-        h_sq(0, 0, 3)
-        e_mm(0, 0)
-        e_mm(0, 1)
-        e_mm(0, 2)
-        e_mm(0, 3)
-        hs_mul(1, 0, 0, 256)
-        hs_mul(1, 0, 256, 512)
-        g_q(1)
-        h_t(0, 1, 0)
-        h_sq(0, 1, 0)
-        h_t(0, 1, 1)
-        h_sq(0, 1, 1)
-        h_t(0, 1, 2)
-        h_sq(0, 1, 2)
-        h_t(0, 1, 3)
-        h_sq(0, 1, 3)
-        e_sub(0, 0)
-        e_sub(0, 1)
-        e_sub(0, 2)
-        e_sub(0, 3)
-        hs_q(0, 1, 0, 512)
-        e_mm(1, 0)
-        e_sub(1, 0)
-        e_mm(1, 1)
-        e_sub(1, 1)
-        e_mm(1, 2)
-        e_sub(1, 2)
-        e_mm(1, 3)
-        e_sub(1, 3)
-        e_q(0)
-        hs_q(1, 0, 0, 512)
-        z_mm(1, 1, 0)
-        tanh(1, 1, 0)
-        z_mm(1, 1, 1)
-        tanh(1, 1, 1)
-        z_mm(1, 1, 2)
-        tanh(1, 1, 2)
-        z_mm(1, 1, 3)
-        tanh(1, 1, 3)
-        h_t(1, 0, 0)
-        h_sq(1, 0, 0)
-        h_t(1, 0, 1)
-        h_sq(1, 0, 1)
-        h_t(1, 0, 2)
-        h_sq(1, 0, 2)
-        h_t(1, 0, 3)
-        h_sq(1, 0, 3)
-        e_q(1)
-        hs_mul(1, 1, 0, 256)
-        hs_mul(1, 1, 256, 512)
-        tau_mm()
-        c_mm(0, 0)
-        c_sq(0, 0)
-        c_mm(0, 1)
-        c_sq(0, 1)
-        c_mm(0, 2)
-        c_sq(0, 2)
-        c_mm(0, 3)
-        c_sq(0, 3)
-        hh_inv(0)
-        hs_q(1, 1, 0, 512)
-        c_out(0, 0, 0, 512)
-        c_out(0, 1, 0, 512)
-        c_out(0, 2, 0, 512)
-        c_out(0, 3, 0, 512)
-        store_o(0, 0, 4)
-        h_t(1, 1, 0)
-        h_sq(1, 1, 0)
-        h_t(1, 1, 1)
-        h_sq(1, 1, 1)
-        h_t(1, 1, 2)
-        h_sq(1, 1, 2)
-        h_t(1, 1, 3)
-        h_sq(1, 1, 3)
-        o_copy(0, 0, 256, "g")
-        c_mm(1, 0)
-        c_sq(1, 0)
-        c_mm(1, 1)
-        c_sq(1, 1)
-        c_mm(1, 2)
-        c_sq(1, 2)
-        c_mm(1, 3)
-        c_sq(1, 3)
-        o_copy(0, 256, 512, "v")
-        hh_inv(1)
-        o_q(0, 256, 512)
-        c_out(1, 0, 0, 512)
-        c_out(1, 1, 0, 512)
-        o_q(0, 0, 256)
-        store_p(0, 0, 512, nc.sync)
-        store_o(1, 0, 2)
-        c_out(1, 2, 0, 512)
-        c_out(1, 3, 0, 512)
-        store_o(1, 2, 4)
-        o_copy(1, 0, 256, "s")
-        o_copy(1, 256, 512, "v")
-        o_q(1, 256, 512)
-        o_q(1, 0, 256)
-        store_p(1, 0, 512, nc.scalar)
+        def quantize_scores(F, half):
+            cols = slice(256 * half, 256 * (half + 1))
+            quantize(
+                out_code[F][:, cols], out_scale[:, F, cols], out_bf[F][:, cols, :].rearrange("p q j -> p (q j)")
+            )
+
+        def store_codes(F):
+            nc.sync.dma_start(
+                out=out_1[F].rearrange("p m j -> p (m j)").bitcast(I32), in_=out_code[F][:].bitcast(I32)
+            )
+
+        for i in TILES:
+            interleave(nc.scalar, x_bf[0], i, turn_x(0, i))
+            quantize_x(0, i, i + 1)
+        for i in TILES:
+            regroup_x(i)
+        nodes(0, 0)
+        for i in TILES:
+            interleave(nc.vector if i < 2 else nc.scalar, x_bf[1], i, turn_x(1, i))
+        gain_nodes(0, 0, 0)
+        quantize_x(1, 0, 2)
+        gain_nodes(0, 0, 1)
+        quantize_x(1, 2, 4)
+        nodes(0, 1)
+        for pair in range(2):
+            interleave(nc.scalar, g_bf[0], pair, turn_g(0, pair))
+        gain_nodes(0, 1, 0)
+        gain_nodes(0, 1, 1)
+        nodes(1, 0)
+        quantize_hs(0, 0)
+        quantize_g(0)
+        for pair in range(2):
+            interleave(nc.scalar, g_bf[1], pair, turn_g(1, pair))
+        node_energy(0, 0)
+        net = [network(0, n) for n in range(4)]
+        gain_nodes(1, 0, 0)
+        gain_nodes(1, 0, 1)
+        quantize_g(1)
+        node_energy(0, 1)
+        for n in range(4):
+            residual(0, n, net[n])
+        quantize_hs(0, 1)
+        for n in range(4):
+            residual(1, n, network(1, n))
+        quantize_e(0)
+        quantize_hs(1, 0)
+        nodes(1, 1)
+        node_energy(1, 0)
+        quantize_e(1)
+        gain_nodes(1, 1, 0)
+        gain_nodes(1, 1, 1)
+        tau_bank = bank()
+        nc.tensor.matmul(tau_bank[:], lhsT=ones[:], rhs=tau_row[:], start=True, stop=True)
+        correlate(0)
+        invert_energy(0)
+        quantize_hs(1, 1)
+        for j in TILES:
+            score(0, j)
+        store_scores(0, 0, 4)
+        node_energy(1, 1)
+        correlate(1)
+        round_scores(nc.vector, 0, 0)
+        invert_energy(1)
+        quantize_scores(0, 0)
+        for j in TILES:
+            score(1, j)
+            if j % 2 == 1:
+                store_scores(1, j - 1, j + 1)
+        round_scores(nc.scalar, 0, 1)
+        round_scores(nc.scalar, 1, 0)
+        round_scores(nc.vector, 1, 1)
+        quantize_scores(0, 1)
+        store_codes(0)
+        quantize_scores(1, 1)
+        quantize_scores(1, 0)
+        store_codes(1)
+        for quad in range(4):
+            nc.scalar.dma_start(
+                out=out_2.rearrange("k b m -> b k m")[4 * quad : 4 * quad + 4, :, :].bitcast(I32),
+                in_=out_scale[32 * quad : 32 * quad + 4, :, :].bitcast(I32),
+            )

from contextlib import ExitStack

import concourse.mybir as mybir
from concourse.masks import make_identity

N, D, H, L, Q = 1024, 1024, 1024, 512, 512
FLOPS = 2 * (N * D * H + N * L * Q + H * N * Q)

F32 = mybir.dt.float32
BF16 = mybir.dt.bfloat16
I32 = mybir.dt.int32
U32 = mybir.dt.uint32
U8 = mybir.dt.uint8
FP8X4 = mybir.dt.float8_e4m3fn_x4
FP4X4 = mybir.dt.float4_e2m1fn_x4
ACT = mybir.ActivationFunctionType
ALU = mybir.AluOpType

P = 128
T = 4
GROUP = P * T
BANK = 512
GROUPS = range(2)
TILES = range(T)


def tile_stochasticconfigurationcandidatescores_x2_kernel(
    tc, x, w_words, w_scales, s, t, g, beta_words, beta_scales, tau, out_0, out_1, out_2
):
    nc = tc.nc
    with ExitStack() as ctx:
        keep = ctx.enter_context(tc.tile_pool(name="keep", bufs=1))
        psum = ctx.enter_context(tc.psum_pool(name="psum", bufs=8))
        ctx.enter_context(tc.manual_schedule())

        def sbuf(name, shape, dtype):
            return keep.tile(shape, dtype, name=name, align_bytes=64)

        def bank():
            return psum.tile([P, BANK], F32, name="bank")

        x_in = [sbuf(f"x_in{G}", [P, T, D], BF16) for G in GROUPS]
        x_words = sbuf("x_words", [P, T, BANK], I32)
        g_in = [sbuf(f"g_in{G}", [P, T, L], BF16) for G in GROUPS]
        t_in = [sbuf(f"t_in{G}", [P, T, Q], BF16) for G in GROUPS]
        w_code = sbuf("w_code", [P, 2, 2 * H], U8)
        w_scale = sbuf("w_scale", [P, 2, H], U8)
        beta_code = sbuf("beta_code", [P, 2 * Q], U8)
        beta_scale = sbuf("beta_scale", [P, Q], U8)
        gain = sbuf("gain", [P, 2, T], BF16)
        tau_row = sbuf("tau_row", [P, Q], BF16)
        ones = sbuf("ones", [P, P], BF16)
        ident = sbuf("ident", [P, P], F32)
        zero = sbuf("zero", [P, 1], F32)

        x_bf = [sbuf(f"x_bf{G}", [P, T * 2 * GROUP], BF16) for G in GROUPS]
        x_code = [sbuf(f"x_code{G}", [P, T, 2, P], U32) for G in GROUPS]
        x_scale = [sbuf(f"x_scale{G}", [P, T, 2, P], U8) for G in GROUPS]
        g_bf = [sbuf(f"g_bf{G}", [P, T * GROUP], BF16) for G in GROUPS]
        g_code = [sbuf(f"g_code{G}", [P, T, P], U32) for G in GROUPS]
        g_scale = [sbuf(f"g_scale{G}", [P, T, P], U8) for G in GROUPS]
        h = [[sbuf(f"h{G}{F}", [P, T, GROUP], F32) for F in GROUPS] for G in GROUPS]
        hs_bf = [[sbuf(f"hs_bf{G}{F}", [P, GROUP, T], BF16) for F in GROUPS] for G in GROUPS]
        hs_code = [[sbuf(f"hs_code{G}{F}", [P, GROUP], U32) for F in GROUPS] for G in GROUPS]
        hs_scale = [[sbuf(f"hs_scale{G}{F}", [P, GROUP], U8) for F in GROUPS] for G in GROUPS]
        e_bf = [sbuf(f"e_bf{G}", [P, Q, T], BF16) for G in GROUPS]
        e_code = [sbuf(f"e_code{G}", [P, Q], U32) for G in GROUPS]
        e_scale = [sbuf(f"e_scale{G}", [P, Q], U8) for G in GROUPS]

        squares = [sbuf(f"squares{i}", [P, BANK], F32) for i in range(2)]
        energy = sbuf("energy", [P, 2, 2 * T], F32)
        hh = sbuf("hh", [P, 2 * T], F32)
        inv_hh = sbuf("inv_hh", [P, 2 * T], F32)
        c_sq = [sbuf(f"c_sq{F}", [P, T, Q], F32) for F in GROUPS]
        out_f32 = [sbuf(f"out_f32{F}", [P, T, Q], F32) for F in GROUPS]
        out_bf = [sbuf(f"out_bf{F}", [P, Q, T], BF16) for F in GROUPS]
        out_code = [sbuf(f"out_code{F}", [P, Q], U32) for F in GROUPS]
        out_scale = sbuf("out_scale", [P, 2, Q], U8)

        nc.vector.memset(zero[:], 0.0)
        nc.vector.memset(w_scale[:].rearrange("p k n -> p (k n)").bitcast(I32), 0)
        nc.vector.memset(beta_scale[:].bitcast(I32), 0)
        nc.vector.memset(ones[:], 1.0)
        make_identity(nc, ident[:])
        nc.gpsimd.memset(tau_row[:], 0.0)

        x_hbm = x.rearrange("(G p i) d -> G p i d", G=2, i=T)
        g_hbm = g.rearrange("(G p i) d -> G p i d", G=2, i=T)
        t_hbm = t.rearrange("(G p i) d -> G p i d", G=2, i=T)
        w_hbm = w_words.rearrange("k p n -> p k n").bitcast(I32)
        w_scale_hbm = w_scales.rearrange("k b n -> b k n").bitcast(I32)

        def load_x(G, lo, hi):
            nc.sync.dma_start(out=x_in[G][:, lo:hi, :], in_=x_hbm[G][:, lo:hi, :])

        def load_w(F):
            nc.sync.dma_start(
                out=w_code[:].bitcast(I32)[:, :, 256 * F : 256 * (F + 1)], in_=w_hbm[:, :, 256 * F : 256 * (F + 1)]
            )

        for quad in range(4):
            nc.scalar.dma_start(
                out=w_scale[32 * quad : 32 * quad + 4, :, :].bitcast(I32),
                in_=w_scale_hbm[4 * quad : 4 * quad + 4, :, :],
            )
        load_x(0, 0, 1)
        load_w(0)
        load_x(0, 1, 2)
        load_x(0, 2, 4)
        load_x(1, 0, 2)
        load_x(1, 2, 4)
        load_w(1)
        nc.sync.dma_start(out=gain[:], in_=s.rearrange("(G p i) -> p G i", G=2, i=T))
        nc.sync.dma_start(out=g_in[0][:], in_=g_hbm[0])
        for quad in range(4):
            nc.sync.dma_start(
                out=beta_scale[32 * quad : 32 * quad + 4, :].bitcast(I32),
                in_=beta_scales[0][4 * quad : 4 * quad + 4, :].bitcast(I32),
            )
        nc.sync.dma_start(out=beta_code[:].bitcast(I32), in_=beta_words[0].bitcast(I32))
        nc.sync.dma_start(out=g_in[1][:], in_=g_hbm[1])
        nc.sync.dma_start(out=t_in[0][:], in_=t_hbm[0])
        nc.sync.dma_start(out=t_in[1][:], in_=t_hbm[1])
        nc.sync.dma_start(out=tau_row[0:1, :], in_=tau.unsqueeze(0))

        nc.scalar.activation(out=zero[:], in_=zero[:], func=ACT.Tanh)

        def copy(eng, out, in_):
            if eng is nc.scalar:
                nc.scalar.copy(out=out, in_=in_)
            else:
                nc.vector.tensor_copy(out=out, in_=in_)

        def quantize(code, scale, in_):
            nc.vector.quantize_mx(out=code.bitcast(FP8X4), scales=scale, in_=in_)

        def regroup_x(i):
            nc.gpsimd.tensor_copy(
                out=x_words[:, i, :].rearrange("p (k u r) -> p k u r", k=2, u=2),
                in_=x_in[1][:, i, :].bitcast(I32).rearrange("p (k r u) -> p k u r", k=2, u=2),
            )

        def turn_x(G, i):
            b = bank()
            words = x_in[G][:, i, :].bitcast(F32)
            for k in range(2):
                for u in range(2):
                    n = 2 * k + u
                    if G == 0:
                        src = words[:, 256 * k + u : 256 * (k + 1) : 2]
                    else:
                        src = x_words[:, i, P * n : P * (n + 1)].bitcast(F32)
                    nc.tensor.transpose(b[:, P * n : P * (n + 1)], src, ident[:])
            return b

        def turn_g(G, pair):
            b = bank()
            for n in range(4):
                words = g_in[G][:, 2 * pair + n // 2, :].bitcast(F32)
                nc.tensor.transpose(b[:, P * n : P * (n + 1)], words[:, n % 2 : 256 : 2], ident[:])
            return b

        def interleave(eng, bf, n, b):
            copy(
                eng,
                out=bf[:].bitcast(F32)[:, BANK * n : BANK * (n + 1)].rearrange("p (a r u) -> p a r u", a=2, u=2),
                in_=b[:].rearrange("p (a u r) -> p a r u", a=2, u=2),
            )

        def quantize_x(G, lo, hi):
            quantize(
                x_code[G][:, lo:hi].rearrange("p i k r -> p (i k r)"),
                x_scale[G][:, lo:hi].rearrange("p i k r -> p (i k r)"),
                x_bf[G][:, 2 * GROUP * lo : 2 * GROUP * hi],
            )

        def quantize_g(G):
            quantize(
                g_code[G][:].rearrange("p i r -> p (i r)"), g_scale[G][:].rearrange("p i r -> p (i r)"), g_bf[G][:]
            )

        def nodes(G, F):
            for i in TILES:
                b = bank()
                for k in range(2):
                    nc.tensor.matmul_mx(
                        out=b[:],
                        lhsT=x_code[G][:, i, k, :].bitcast(FP8X4),
                        lhsT_scale=x_scale[G][:, i, k, :],
                        rhs=w_code[:, k, H * F : H * (F + 1)].bitcast(FP4X4),
                        rhs_scale=w_scale[:, k, GROUP * F : GROUP * (F + 1)],
                        start=(k == 0),
                        stop=(k == 1),
                    )
                nc.scalar.activation(
                    out=h[G][F][:, i, :].rearrange("p (j m) -> p j m", j=T),
                    in_=b[:].rearrange("p (m j) -> p j m", j=T),
                    func=ACT.Tanh,
                    bias=zero[:, 0:1],
                )

        def gain_nodes(G, F, half):
            cols = slice(256 * half, 256 * (half + 1))
            nc.vector.tensor_tensor(
                out=hs_bf[G][F][:, cols, :].rearrange("p (c f) i -> p c i f", f=4),
                in0=h[G][F][:, :, cols].rearrange("p i (c f) -> p c i f", f=4),
                in1=gain[:, G, :].unsqueeze(1).unsqueeze(3).to_broadcast([P, 64, T, 4]),
                op=ALU.mult,
            )

        def quantize_hs(G, F):
            quantize(hs_code[G][F][:], hs_scale[G][F][:], hs_bf[G][F][:].rearrange("p f i -> p (f i)"))

        def node_energy(G, F):
            for j in TILES:
                b = bank()
                for i in TILES:
                    nc.tensor.transpose(b[:, P * i : P * (i + 1)], h[G][F][:, i, P * j : P * (j + 1)], ident[:])
                n = T * F + j
                nc.scalar.activation(
                    out=squares[j % 2][:], in_=b[:], func=ACT.Square, accum_out=energy[:, G, n : n + 1]
                )

        def invert_energy(F):
            cols = slice(T * F, T * (F + 1))
            nc.vector.tensor_tensor(out=hh[:, cols], in0=energy[:, 0, cols], in1=energy[:, 1, cols], op=ALU.add)
            nc.vector.reciprocal(out=inv_hh[:, cols], in_=hh[:, cols])

        def network(G, n):
            b = bank()
            for i in TILES:
                nc.tensor.matmul_mx(
                    out=b[:, P * i : P * (i + 1)],
                    lhsT=g_code[G][:, i, :].bitcast(FP8X4),
                    lhsT_scale=g_scale[G][:, i, :],
                    rhs=beta_code[:, 2 * P * n : 2 * P * (n + 1)].bitcast(FP4X4),
                    rhs_scale=beta_scale[:, P * n : P * (n + 1)],
                    start=True,
                    stop=True,
                )
            return b

        def residual(G, n, b):
            cols = slice(P * n, P * (n + 1))
            nc.vector.tensor_tensor(
                out=e_bf[G][:, cols, :].rearrange("p (c q) i -> p c i q", q=4),
                in0=t_in[G][:, :, cols].rearrange("p i (c q) -> p c i q", q=4),
                in1=b[:].rearrange("p (i c q) -> p c i q", i=T, q=4),
                op=ALU.subtract,
            )

        def quantize_e(G):
            quantize(e_code[G][:], e_scale[G][:], e_bf[G][:].rearrange("p q i -> p (q i)"))

        def correlate(F):
            for j in TILES:
                b = bank()
                for G in GROUPS:
                    nc.tensor.matmul_mx(
                        out=b[:],
                        lhsT=hs_code[G][F][:, P * j : P * (j + 1)].bitcast(FP8X4),
                        lhsT_scale=hs_scale[G][F][:, P * j : P * (j + 1)],
                        rhs=e_code[G][:].bitcast(FP8X4),
                        rhs_scale=e_scale[G][:],
                        start=(G == 0),
                        stop=(G == 1),
                    )
                nc.scalar.activation(out=c_sq[F][:, j, :], in_=b[:], func=ACT.Square)

        def score(F, j):
            n = T * F + j
            nc.vector.scalar_tensor_tensor(
                out=out_f32[F][:, j, :],
                in0=c_sq[F][:, j, :],
                scalar=inv_hh[:, n : n + 1],
                in1=tau_bank[:],
                op0=ALU.mult,
                op1=ALU.subtract,
            )

        def store_scores(F, lo, hi):
            nc.sync.dma_start(
                out=out_0[GROUP * F : GROUP * (F + 1), :].rearrange("(p j) q -> p j q", j=T)[:, lo:hi, :],
                in_=out_f32[F][:, lo:hi, :],
            )

        def round_scores(eng, F, half):
            cols = slice(256 * half, 256 * (half + 1))
            copy(
                eng,
                out=out_bf[F][:, cols, :].rearrange("p (c q) j -> p c j q", q=4),
                in_=out_f32[F][:, :, cols].rearrange("p j (c q) -> p c j q", q=4),
            )

        def quantize_scores(F, half):
            cols = slice(256 * half, 256 * (half + 1))
            quantize(
                out_code[F][:, cols], out_scale[:, F, cols], out_bf[F][:, cols, :].rearrange("p q j -> p (q j)")
            )

        def store_codes(F):
            nc.sync.dma_start(
                out=out_1[F].rearrange("p m j -> p (m j)").bitcast(I32), in_=out_code[F][:].bitcast(I32)
            )

        for i in TILES:
            interleave(nc.scalar, x_bf[0], i, turn_x(0, i))
            quantize_x(0, i, i + 1)
        for i in TILES:
            regroup_x(i)
        nodes(0, 0)
        for i in TILES:
            interleave(nc.vector if i < 2 else nc.scalar, x_bf[1], i, turn_x(1, i))
        gain_nodes(0, 0, 0)
        quantize_x(1, 0, 2)
        gain_nodes(0, 0, 1)
        quantize_x(1, 2, 4)
        nodes(0, 1)
        for pair in range(2):
            interleave(nc.scalar, g_bf[0], pair, turn_g(0, pair))
        gain_nodes(0, 1, 0)
        gain_nodes(0, 1, 1)
        nodes(1, 0)
        quantize_hs(0, 0)
        quantize_g(0)
        for pair in range(2):
            interleave(nc.scalar, g_bf[1], pair, turn_g(1, pair))
        node_energy(0, 0)
        net = [network(0, n) for n in range(4)]
        gain_nodes(1, 0, 0)
        gain_nodes(1, 0, 1)
        quantize_g(1)
        node_energy(0, 1)
        for n in range(4):
            residual(0, n, net[n])
        quantize_hs(0, 1)
        for n in range(4):
            residual(1, n, network(1, n))
        quantize_e(0)
        quantize_hs(1, 0)
        nodes(1, 1)
        node_energy(1, 0)
        quantize_e(1)
        gain_nodes(1, 1, 0)
        gain_nodes(1, 1, 1)
        tau_bank = bank()
        nc.tensor.matmul(tau_bank[:], lhsT=ones[:], rhs=tau_row[:], start=True, stop=True)
        correlate(0)
        invert_energy(0)
        quantize_hs(1, 1)
        for j in TILES:
            score(0, j)
        store_scores(0, 0, 4)
        node_energy(1, 1)
        correlate(1)
        round_scores(nc.vector, 0, 0)
        invert_energy(1)
        quantize_scores(0, 0)
        for j in TILES:
            score(1, j)
            if j % 2 == 1:
                store_scores(1, j - 1, j + 1)
        round_scores(nc.scalar, 0, 1)
        round_scores(nc.scalar, 1, 0)
        round_scores(nc.vector, 1, 1)
        quantize_scores(0, 1)
        store_codes(0)
        quantize_scores(1, 1)
        quantize_scores(1, 0)
        store_codes(1)
        for quad in range(4):
            nc.scalar.dma_start(
                out=out_2.rearrange("k b m -> b k m")[4 * quad : 4 * quad + 4, :, :].bitcast(I32),
                in_=out_scale[32 * quad : 32 * quad + 4, :, :].bitcast(I32),
            )
